import numpy as np
import ml_dtypes


def mxq(x, axis, fmt="e4m3"):
    dtype, down = {"e4m3": (ml_dtypes.float8_e4m3fn, 7), "e5m2": (ml_dtypes.float8_e5m2, 14)}[fmt]
    v = np.moveaxis(np.asarray(x, np.float32).astype(ml_dtypes.bfloat16).astype(np.float64), axis, -1)
    blocks = v.reshape(v.shape[:-1] + (-1, 32))
    amax = np.abs(blocks).max(-1, keepdims=True)
    byte = np.maximum(np.where(amax > 0, np.frexp(amax)[1] - 1 + 127, 0) - down, 1)
    scale = np.exp2(byte - 127.0)
    codes = (blocks / scale).astype(np.float32).astype(dtype).astype(np.float64)
    return np.moveaxis((codes * scale).reshape(v.shape), -1, axis)


WIDE = False


def mx_kscale(k):
    if not WIDE:
        return np.ones(k)
    levels = np.array([10, -10, 5, -5, 0])
    if k % 512:
        return np.exp2(np.random.permutation(np.resize(levels, k // 32))).repeat(32)
    a = np.empty((k // 512, 16))
    for p in range(k // 512):
        a[p, :8] = np.random.permutation(np.resize(levels, 8))
        for g in range(8):
            far = levels[np.abs(levels - a[p, g]) >= 10]
            a[p, g + 8] = far[np.random.randint(len(far))]
    return np.exp2(a.ravel()).repeat(32)


def f64(x):
    return np.asarray(x).astype(np.float64)


def striped(idx):
    return np.tile(idx.reshape(-1, 16).T, (8, 1)).astype(np.uint16)


def unstriped(offs):
    return offs[:16].T.reshape(-1).astype(np.int64)


E2M1 = np.array([0.0, 0.5, 1.0, 1.5, 2.0, 3.0, 4.0, 6.0, -0.0, -0.5, -1.0, -1.5, -2.0, -3.0, -4.0, -6.0])


def pack_weight(w, fmt):
    k, n = w.shape
    w = f64(np.asarray(w, np.float32).astype(ml_dtypes.bfloat16)).reshape(k // 32, 32, n)
    amax = np.abs(w).max(1)
    if fmt == "e4m3":
        byte = np.frexp(amax)[1] - 1 + 127 - 7
    else:
        mant, ex = np.frexp(amax / 6.0)
        byte = np.where(mant > 0.5, ex, ex - 1) + 127
    byte = np.clip(np.where(amax > 0, byte, 1), 1, 254)
    scaled = (w * np.exp2(127.0 - byte)[:, None, :]).reshape(k, n).astype(np.float32)
    by_word = np.ascontiguousarray(scaled.reshape(k // 512, 128, 4, n).transpose(0, 1, 3, 2))
    if fmt == "e4m3":
        words = by_word.astype(ml_dtypes.float8_e4m3fn).view(np.uint8)
    else:
        c = by_word.astype(ml_dtypes.float4_e2m1fn).view(np.uint8) & 0xF
        words = (c[..., 0::2] | (c[..., 1::2] << 4)).reshape(k // 512, 128, 2 * n)
    return np.ascontiguousarray(words), np.ascontiguousarray(byte.astype(np.uint8).reshape(k // 512, 16, n))


def unpack_weight(words, scales, fmt):
    g, _, n = scales.shape
    words = np.ascontiguousarray(words).reshape(g, 128, n, -1)
    if fmt == "e4m3":
        vals = words.view(ml_dtypes.float8_e4m3fn).astype(np.float64)
    else:
        nib = np.empty((g, 128, n, 4), np.uint8)
        nib[..., 0::2] = words & 0xF
        nib[..., 1::2] = words >> 4
        vals = E2M1[nib]
    vals = vals * np.repeat(np.exp2(scales.astype(np.float64) - 127.0), 8, axis=1)[..., None]
    return vals.transpose(0, 1, 3, 2).reshape(g * 512, n)


def gelu(v):
    return 0.5 * v * (1.0 + np.tanh(np.sqrt(2.0 / np.pi) * (v + 0.044715 * v**3)))


def bf(x):
    return np.asarray(x, np.float32).astype(ml_dtypes.bfloat16)


def planes(Y):
    n, m = Y.shape
    b = f64(bf(Y)).reshape(n // 32, 32, m)
    amax = np.abs(b).max(1)
    byte = np.clip(np.where(amax > 0, np.frexp(amax)[1] - 1 + 127 - 7, 1), 1, 254)
    codes = (b * np.exp2(127.0 - byte)[:, None, :]).reshape(n, m).astype(np.float32).astype(ml_dtypes.float8_e4m3fn).view(np.uint8)
    words = codes.reshape(n // 512, 128, 4, m).transpose(0, 1, 3, 2)
    return np.ascontiguousarray(words), np.ascontiguousarray(byte.astype(np.uint8).reshape(n // 512, 16, m))


K, H, N, T, S, T2 = 1024, 1024, 512, 2048, 1024, 2048

def setup_inputs():
    n = np.random.standard_normal
    s = mx_kscale(K)[:, None]
    u = mx_kscale(H)[:, None]
    tab_words, tab_scales = pack_weight(n((K, T)) * s, "e4m3")
    w2_words, w2_scales = pack_weight(n((H, N)) / np.sqrt(H) / u, "e2m1")
    return {
        "tab_words": tab_words, "tab_scales": tab_scales,
        "offs": striped(np.random.permutation(T)[:S]),
        "offs2": striped(np.random.permutation(T2)[:S]),
        "w1": (n((K, H)) / np.sqrt(K) / s * u.T).astype(np.float32),
        "right": (0.5 * n((H, S)) / u).astype(np.float32),
        "wgs": np.exp(0.3 * n((128, S))).astype(np.float32),
        "page0": (n((H, T2)) * u).astype(np.float32),
        "w2_words": w2_words, "w2_scales": w2_scales,
    }

def reference(tab_words, tab_scales, offs, offs2, w1, right, wgs, page0, w2_words, w2_scales):
    v = unpack_weight(tab_words, tab_scales, "e4m3")[:, unstriped(offs)]
    left = mxq(f64(w1), 0, "e4m3").T @ v
    h = np.square(left) * f64(right) - left
    page = f64(page0).copy()
    page[:, unstriped(offs2)] = np.tile(f64(wgs), (H // 128, 1)) * h
    words, scales = planes(page)
    w2 = unpack_weight(w2_words, w2_scales, "e2m1")
    prod = w2.T @ mxq(page, 0, "e4m3")
    y = np.log(1.0 + np.square(prod))
    return y, page, words, scales

@@ -1,0 +1,259 @@
+from contextlib import ExitStack
+
+import concourse.mybir as mybir
+
+K, H, N, T, S, T2 = 1024, 1024, 512, 2048, 1024, 2048
+FLOPS = 2 * K * H * S + 2 * H * N * T2
+
+F32 = mybir.dt.float32
+BF16 = mybir.dt.bfloat16
+I32 = mybir.dt.int32
+U32 = mybir.dt.uint32
+U16 = mybir.dt.uint16
+U8 = mybir.dt.uint8
+FP8X4 = mybir.dt.float8_e4m3fn_x4
+FP4X4 = mybir.dt.float4_e2m1fn_x4
+ALU = mybir.AluOpType
+ACT = mybir.ActivationFunctionType
+
+P = 128
+BANK = 512
+QUADS = (0, 2, 1, 3)
+GP_TILES = (1, 2, 3, 4, 5, 6, 7)
+
+
+def tile_list_turf_probe_page_kernel(
+    tc, tab_words, tab_scales, offs, offs2, w1, right, wgs, page0, w2_words, w2_scales, out_0, out_1, out_2, out_3
+):
+    nc = tc.nc
+    with ExitStack() as ctx:
+        lists = ctx.enter_context(tc.tile_pool(name="lists", bufs=1))
+        sb = ctx.enter_context(tc.tile_pool(name="sb", bufs=1))
+        ring = ctx.enter_context(tc.tile_pool(name="ring", bufs=2))
+        psum = ctx.enter_context(tc.psum_pool(name="psum", bufs=1))
+
+        def tile(shape, dtype, name, tag=None):
+            return sb.tile(shape, dtype, name=name, tag=tag or name, align_bytes=64)
+
+        idx = lists.tile([P, S // 16], U16, name="idx")
+        idx2 = lists.tile([P, S // 16], U16, name="idx2")
+        tabw = [tile([P, T], U32, "tabw%d" % a) for a in range(2)]
+        tabs = tile([P, T], U8, "tabs")
+        w1raw = [[tile([P, 4, 512], F32, "w1raw%d%d" % (g, a)) for a in range(2)] for g in range(2)]
+        rt = [tile([P, S], F32, "right%d" % i) for i in range(8)]
+        wg01 = [tile([P, S], F32, "wg%d" % t) for t in range(2)]
+        wg23 = tile([P, 2, S], F32, "wg23")
+        wg = [wg01[0][:], wg01[1][:], wg23[:, 0, :], wg23[:, 1, :]]
+        page = [tile([P, T2], F32, "page%d" % i) for i in range(8)]
+        w2w = tile([P, 2, 2 * N], U8, "w2w")
+        w2s = tile([P, 2, N], U8, "w2s")
+        warm = tile([P, 1], F32, "warm")
+
+        rows_right = right.rearrange("(g p t) j -> g t p j", g=2, t=4)
+        rows_page0 = page0.rearrange("(g p t) m -> g t p m", g=2, t=4)
+        rows_out1 = out_1.rearrange("(g p t) m -> g t p m", g=2, t=4)
+        rows_wgs = wgs.rearrange("(q t) j -> q t j", t=4)
+
+        nc.vector.memset(tabs[:].bitcast(I32), 0)
+        nc.vector.memset(w2s[:].rearrange("p a c -> p (a c)").bitcast(I32), 0)
+        nc.vector.memset(warm[:], 1.0)
+
+        def load_tabw(a):
+            nc.sync.dma_start(tabw[a][:].bitcast(I32), tab_words[a].rearrange("p t i -> p (t i)").bitcast(I32))
+
+        def load_w1(g, a):
+            src = w1[512 * a : 512 * (a + 1), 512 * g : 512 * (g + 1)].rearrange("(p j) c -> p j c", j=4)
+            nc.sync.dma_start(w1raw[g][a][:], src)
+
+        def load_right(i):
+            nc.sync.dma_start(rt[i][:], rows_right[i // 4, i % 4])
+
+        def load_page(i):
+            nc.sync.dma_start(page[i][:], rows_page0[i // 4, i % 4])
+
+        def load_wg(t):
+            for q in QUADS:
+                nc.sync.dma_start(wg01[t][32 * q : 32 * (q + 1), :], rows_wgs[:, t, :])
+
+        load_tabw(0)
+        nc.sync.dma_start(idx[:], offs)
+        for q in range(4):
+            nc.scalar.dma_start(
+                tabs[32 * q : 32 * q + 8, :].bitcast(I32), tab_scales[:, 4 * q : 4 * q + 4, :].bitcast(I32)
+            )
+        nc.scalar.activation(warm[:], warm[:], ACT.Ln)
+        load_w1(0, 0)
+        load_tabw(1)
+        load_w1(0, 1)
+        nc.sync.dma_start(idx2[:], offs2)
+        load_right(0)
+        load_wg(0)
+        load_page(0)
+        load_right(1)
+        load_wg(1)
+        load_page(1)
+        load_right(2)
+        for q in QUADS:
+            nc.sync.dma_start(wg23[32 * q : 32 * (q + 1), :, :], rows_wgs[:, 2:4, :])
+        load_right(3)
+        load_w1(1, 0)
+        load_w1(1, 1)
+        load_page(2)
+        load_page(3)
+        for i in range(4, 8):
+            load_right(i)
+            load_page(i)
+        nc.sync.dma_start(w2w[:].bitcast(I32), w2_words.rearrange("a p c -> p a c").bitcast(I32))
+        for q in range(4):
+            nc.sync.dma_start(
+                w2s[32 * q : 32 * q + 4, :, :].bitcast(I32),
+                w2_scales[:, 4 * q : 4 * q + 4, :].rearrange("a r c -> r a c").bitcast(I32),
+            )
+
+        gs = tile([P, S], U8, "gs")
+        gw = [tile([P, S], U32, "gw%d" % a) for a in range(2)]
+        nc.vector.tensor_copy(gs[:], tabs[:].indirect(idx[:]))
+        w1c = [[tile([P, 512], U32, "w1c%d%d" % (g, a)) for a in range(2)] for g in range(2)]
+        w1s = [[tile([P, 512], U8, "w1s%d%d" % (g, a)) for a in range(2)] for g in range(2)]
+
+        def quant_w1(g, a, on_vector):
+            dealt = ring.tile([P, 2048], BF16, name="w1bf", tag="bf", align_bytes=64)
+            dst = dealt[:].rearrange("p (t m j) -> p m j t", t=4, j=4)
+            src = w1raw[g][a][:].rearrange("p j (m t) -> p m j t", t=4)
+            if on_vector:
+                nc.vector.tensor_copy(dst, src)
+            else:
+                nc.scalar.copy(dst, src)
+            nc.vector.quantize_mx(out=w1c[g][a][:].bitcast(FP8X4), scales=w1s[g][a][:], in_=dealt[:])
+
+        nc.vector.tensor_copy(gw[0][:], tabw[0][:].indirect(idx[:]))
+        quant_w1(0, 0, False)
+        nc.vector.tensor_copy(gw[1][:], tabw[1][:].indirect(idx[:]))
+        quant_w1(0, 1, True)
+
+        codes = [tile([P, T2], U32, "codes%d" % g) for g in range(2)]
+        scales = [tile([P, T2], U8, "scales%d" % g) for g in range(2)]
+        widths = [1024, 512]
+        plane_tags = [["tabw0", "tabw1"], ["right0", "right1", "right2", "right3"]]
+        planes = [None, None]
+
+        def left_tile(i):
+            g, t = i // 4, i % 4
+            banks = []
+            for h in range(2):
+                acc = psum.tile([P, BANK], F32, name="left", tag="bank%d" % (2 * (i % 2) + h))
+                for a in range(2):
+                    nc.tensor.matmul_mx(
+                        out=acc[:],
+                        lhsT=w1c[g][a][:, P * t : P * (t + 1)].bitcast(FP8X4),
+                        lhsT_scale=w1s[g][a][:, P * t : P * (t + 1)],
+                        rhs=gw[a][:, BANK * h : BANK * (h + 1)].bitcast(FP8X4),
+                        rhs_scale=gs[4 * a : P, BANK * h : BANK * (h + 1)],
+                        start=(a == 0),
+                        stop=(a == 1),
+                    )
+                banks.append(acc)
+            return banks
+
+        def prepare(i):
+            banks = left_tile(i)
+            r = rt[i]
+            if i in GP_TILES:
+                lc = ring.tile([P, S], F32, name="lc", tag="lc", align_bytes=64)
+                for h in range(2):
+                    nc.scalar.copy(lc[:, BANK * h : BANK * (h + 1)], banks[h][:])
+                nc.gpsimd.tensor_tensor(r[:], lc[:], r[:], ALU.mult)
+                nc.gpsimd.tensor_tensor(lc[:], lc[:], wg[i % 4], ALU.mult)
+                return lc
+            return banks
+
+        def replace(i, made):
+            r = rt[i]
+            if i in GP_TILES:
+                nc.vector.scalar_tensor_tensor(r[:], r[:], -1.0, made[:], ALU.add, ALU.mult)
+                nc.vector.tensor_copy(page[i][:].indirect(idx2[:]), r[:])
+            else:
+                for h in range(2):
+                    c = slice(BANK * h, BANK * (h + 1))
+                    nc.vector.tensor_tensor(r[:, c], made[h][:], r[:, c], ALU.mult)
+                for h in range(2):
+                    c = slice(BANK * h, BANK * (h + 1))
+                    nc.vector.scalar_tensor_tensor(r[:, c], r[:, c], -1.0, made[h][:], ALU.add, ALU.mult)
+                nc.vector.tensor_tensor(page[i][:].indirect(idx2[:]), r[:], wg[i % 4], ALU.mult)
+            nc.sync.dma_start(rows_out1[i // 4, i % 4], page[i][:])
+
+        def round_plane(i):
+            g, t = i // 4, i % 4
+            w = widths[g]
+            if t == 0:
+                planes[g] = [
+                    tile([P, 4, w], BF16, "plane%d%d" % (g, c), tag=plane_tags[g][c]) for c in range(T2 // w)
+                ]
+            for c in range(T2 // w):
+                nc.scalar.copy(planes[g][c][:, t, :], page[i][:, w * c : w * (c + 1)])
+
+        def quant_page(g):
+            w = widths[g]
+            for c in range(T2 // w):
+                if g == 0:
+                    woven = tile([P, 4 * w], BF16, "woven%d" % c, tag="w1raw0%d" % c)
+                else:
+                    woven = ring.tile([P, 4 * w], BF16, name="woven", tag="bf", align_bytes=64)
+                dst = woven[:].rearrange("p (c i t) -> p c t i", i=4, t=4)
+                src = planes[g][c][:].rearrange("p t (c i) -> p c t i", i=4)
+                if g == 0:
+                    nc.scalar.copy(dst, src)
+                else:
+                    nc.vector.tensor_copy(dst, src)
+                cols = slice(w * c, w * (c + 1))
+                nc.vector.quantize_mx(out=codes[g][:, cols].bitcast(FP8X4), scales=scales[g][:, cols], in_=woven[:])
+                nc.sync.dma_start(
+                    out_2[g].rearrange("p m t -> p (m t)").bitcast(I32)[:, cols], codes[g][:, cols].bitcast(I32)
+                )
+            for q in range(4):
+                nc.sync.dma_start(
+                    out_3[g, 4 * q : 4 * q + 4, :].bitcast(I32), scales[g][32 * q : 32 * q + 4, :].bitcast(I32)
+                )
+
+        made = {0: prepare(0), 1: prepare(1)}
+        for i in range(8):
+            replace(i, made[i])
+            if i == 0:
+                quant_w1(1, 0, False)
+                quant_w1(1, 1, False)
+            if i + 2 < 8:
+                made[i + 2] = prepare(i + 2)
+            round_plane(i)
+            if i == 5:
+                quant_page(0)
+        quant_page(1)
+
+        stage_tags = ["w1raw10", "w1raw11", "w1raw00", "w1raw01"]
+        rows_out0 = out_0.rearrange("(n p) m -> p n m", p=P)
+        for c in range(4):
+            cols = slice(BANK * c, BANK * (c + 1))
+            staged = tile([P, 4, BANK], F32, "staged%d" % c, tag=stage_tags[c])
+            for n in range(4):
+                k = 4 * c + n
+                acc = psum.tile([P, BANK], F32, name="prod", tag="bank%d" % ((k + 4) % 8))
+                for g in range(2):
+                    nc.tensor.matmul_mx(
+                        out=acc[:],
+                        lhsT=w2w[:, g, 2 * P * n : 2 * P * (n + 1)].bitcast(FP4X4),
+                        lhsT_scale=w2s[:, g, P * n : P * (n + 1)],
+                        rhs=codes[g][:, cols].bitcast(FP8X4),
+                        rhs_scale=scales[g][:, cols],
+                        start=(g == 0),
+                        stop=(g == 1),
+                    )
+                y = staged[:, n, :]
+                if k < 4 or k % 3 == 1:
+                    nc.scalar.activation(y, acc[:], ACT.Square)
+                else:
+                    nc.vector.tensor_copy(y, acc[:])
+                    nc.vector.tensor_tensor(y, acc[:], y, ALU.mult)
+                nc.scalar.activation(y, y, ACT.Ln, bias=1.0)
+                if c == 3:
+                    nc.sync.dma_start(rows_out0[:, n, cols], y)
+                elif n % 2 == 1:
+                    nc.sync.dma_start(rows_out0[:, n - 1 : n + 1, cols], staged[:, n - 1 : n + 1, :])

@@ -19,7 +19,6 @@ ACT = mybir.ActivationFunctionType
 P = 128
 BANK = 512
 QUADS = (0, 2, 1, 3)
-GP_TILES = (1, 2, 3, 4, 5, 6, 7)
 
 
 def tile_list_turf_probe_page_kernel(
@@ -29,7 +28,7 @@ def tile_list_turf_probe_page_kernel(
     with ExitStack() as ctx:
         lists = ctx.enter_context(tc.tile_pool(name="lists", bufs=1))
         sb = ctx.enter_context(tc.tile_pool(name="sb", bufs=1))
-        ring = ctx.enter_context(tc.tile_pool(name="ring", bufs=2))
+        ring = ctx.enter_context(tc.tile_pool(name="ring", bufs=4))
         psum = ctx.enter_context(tc.psum_pool(name="psum", bufs=1))
 
         def tile(shape, dtype, name, tag=None):
@@ -41,9 +40,7 @@ def tile_list_turf_probe_page_kernel(
         tabs = tile([P, T], U8, "tabs")
         w1raw = [[tile([P, 4, 512], F32, "w1raw%d%d" % (g, a)) for a in range(2)] for g in range(2)]
         rt = [tile([P, S], F32, "right%d" % i) for i in range(8)]
-        wg01 = [tile([P, S], F32, "wg%d" % t) for t in range(2)]
-        wg23 = tile([P, 2, S], F32, "wg23")
-        wg = [wg01[0][:], wg01[1][:], wg23[:, 0, :], wg23[:, 1, :]]
+        wg = [tile([P, S], F32, "wg%d" % t) for t in range(4)]
         page = [tile([P, T2], F32, "page%d" % i) for i in range(8)]
         w2w = tile([P, 2, 2 * N], U8, "w2w")
         w2s = tile([P, 2, N], U8, "w2s")
@@ -71,9 +68,9 @@ def tile_list_turf_probe_page_kernel(
         def load_page(i):
             nc.sync.dma_start(page[i][:], rows_page0[i // 4, i % 4])
 
-        def load_wg(t):
+        def load_wg(t, cols=slice(0, S)):
             for q in QUADS:
-                nc.sync.dma_start(wg01[t][32 * q : 32 * (q + 1), :], rows_wgs[:, t, :])
+                nc.sync.dma_start(wg[t][32 * q : 32 * (q + 1), cols], rows_wgs[:, t, cols])
 
         load_tabw(0)
         nc.sync.dma_start(idx[:], offs)
@@ -82,23 +79,24 @@ def tile_list_turf_probe_page_kernel(
                 tabs[32 * q : 32 * q + 8, :].bitcast(I32), tab_scales[:, 4 * q : 4 * q + 4, :].bitcast(I32)
             )
         nc.scalar.activation(warm[:], warm[:], ACT.Ln)
-        load_w1(0, 0)
         load_tabw(1)
+        load_w1(0, 0)
         load_w1(0, 1)
         nc.sync.dma_start(idx2[:], offs2)
         load_right(0)
-        load_wg(0)
+        load_wg(0, slice(0, BANK))
         load_page(0)
-        load_right(1)
+        load_wg(0, slice(BANK, S))
         load_wg(1)
+        load_right(1)
         load_page(1)
+        load_wg(2)
         load_right(2)
-        for q in QUADS:
-            nc.sync.dma_start(wg23[32 * q : 32 * (q + 1), :, :], rows_wgs[:, 2:4, :])
-        load_right(3)
         load_w1(1, 0)
         load_w1(1, 1)
         load_page(2)
+        load_wg(3)
+        load_right(3)
         load_page(3)
         for i in range(4, 8):
             load_right(i)
@@ -113,29 +111,31 @@ def tile_list_turf_probe_page_kernel(
         gs = tile([P, S], U8, "gs")
         gw = [tile([P, S], U32, "gw%d" % a) for a in range(2)]
         nc.vector.tensor_copy(gs[:], tabs[:].indirect(idx[:]))
-        w1c = [[tile([P, 512], U32, "w1c%d%d" % (g, a)) for a in range(2)] for g in range(2)]
+        w1c = {(0, a): tile([P, 512], U32, "w1c0%d" % a)[:] for a in range(2)}
         w1s = [[tile([P, 512], U8, "w1s%d%d" % (g, a)) for a in range(2)] for g in range(2)]
 
-        def quant_w1(g, a, on_vector):
-            dealt = ring.tile([P, 2048], BF16, name="w1bf", tag="bf", align_bytes=64)
-            dst = dealt[:].rearrange("p (t m j) -> p m j t", t=4, j=4)
-            src = w1raw[g][a][:].rearrange("p j (m t) -> p m j t", t=4)
+        def quant_w1(g, a, t0, nt, tag, on_vector):
+            dealt = tile([P, 512 * nt], BF16, "w1bf", tag=tag)
+            dst = dealt[:].rearrange("p (t m j) -> p m j t", t=nt, j=4)
+            src = w1raw[g][a][:].rearrange("p j (m t) -> p m j t", t=4)[:, :, :, t0 : t0 + nt]
             if on_vector:
                 nc.vector.tensor_copy(dst, src)
             else:
                 nc.scalar.copy(dst, src)
-            nc.vector.quantize_mx(out=w1c[g][a][:].bitcast(FP8X4), scales=w1s[g][a][:], in_=dealt[:])
+            cols = slice(P * t0, P * (t0 + nt))
+            nc.vector.quantize_mx(out=w1c[g, a][:, cols].bitcast(FP8X4), scales=w1s[g][a][:, cols], in_=dealt[:])
 
         nc.vector.tensor_copy(gw[0][:], tabw[0][:].indirect(idx[:]))
-        quant_w1(0, 0, False)
         nc.vector.tensor_copy(gw[1][:], tabw[1][:].indirect(idx[:]))
-        quant_w1(0, 1, True)
+        quant_w1(0, 0, 0, 2, "woven0", False)
+        quant_w1(0, 1, 0, 2, "woven1", True)
+        quant_w1(0, 0, 2, 2, "woven2", False)
+        quant_w1(0, 1, 2, 2, "woven3", False)
 
-        codes = [tile([P, T2], U32, "codes%d" % g) for g in range(2)]
+        codes = {}
         scales = [tile([P, T2], U8, "scales%d" % g) for g in range(2)]
         widths = [1024, 512]
-        plane_tags = [["tabw0", "tabw1"], ["right0", "right1", "right2", "right3"]]
-        planes = [None, None]
+        planes = {}
 
         def left_tile(i):
             g, t = i // 4, i % 4
@@ -145,7 +145,7 @@ def tile_list_turf_probe_page_kernel(
                 for a in range(2):
                     nc.tensor.matmul_mx(
                         out=acc[:],
-                        lhsT=w1c[g][a][:, P * t : P * (t + 1)].bitcast(FP8X4),
+                        lhsT=w1c[g, a][:, P * t : P * (t + 1)].bitcast(FP8X4),
                         lhsT_scale=w1s[g][a][:, P * t : P * (t + 1)],
                         rhs=gw[a][:, BANK * h : BANK * (h + 1)].bitcast(FP8X4),
                         rhs_scale=gs[4 * a : P, BANK * h : BANK * (h + 1)],
@@ -155,78 +155,104 @@ def tile_list_turf_probe_page_kernel(
                 banks.append(acc)
             return banks
 
-        def prepare(i):
-            banks = left_tile(i)
-            r = rt[i]
-            if i in GP_TILES:
-                lc = ring.tile([P, S], F32, name="lc", tag="lc", align_bytes=64)
-                for h in range(2):
-                    nc.scalar.copy(lc[:, BANK * h : BANK * (h + 1)], banks[h][:])
-                nc.gpsimd.tensor_tensor(r[:], lc[:], r[:], ALU.mult)
-                nc.gpsimd.tensor_tensor(lc[:], lc[:], wg[i % 4], ALU.mult)
-                return lc
-            return banks
+        halves = [slice(0, BANK), slice(BANK, S)]
 
-        def replace(i, made):
-            r = rt[i]
-            if i in GP_TILES:
-                nc.vector.scalar_tensor_tensor(r[:], r[:], -1.0, made[:], ALU.add, ALU.mult)
-                nc.vector.tensor_copy(page[i][:].indirect(idx2[:]), r[:])
-            else:
-                for h in range(2):
-                    c = slice(BANK * h, BANK * (h + 1))
-                    nc.vector.tensor_tensor(r[:, c], made[h][:], r[:, c], ALU.mult)
-                for h in range(2):
-                    c = slice(BANK * h, BANK * (h + 1))
-                    nc.vector.scalar_tensor_tensor(r[:, c], r[:, c], -1.0, made[h][:], ALU.add, ALU.mult)
-                nc.vector.tensor_tensor(page[i][:].indirect(idx2[:]), r[:], wg[i % 4], ALU.mult)
+        def copy_left(i):
+            banks = left_tile(i)
+            lc = ring.tile([P, S], F32, name="lc", tag="lc", align_bytes=64)
+            for h in range(2):
+                nc.scalar.copy(lc[:, halves[h]], banks[h][:])
+            return lc
+
+        def products(i, lc):
+            lw = tile([P, S], F32, "lw")
+            nc.gpsimd.tensor_tensor(lw[:], lc[:], wg[i % 4][:], ALU.mult)
+            nc.gpsimd.tensor_tensor(lc[:], lc[:], rt[i][:], ALU.mult)
+            return lw
+
+        def replace_first():
+            banks = left_tile(0)
+            r = rt[0]
+            for h in range(2):
+                c = halves[h]
+                nc.vector.tensor_tensor(r[:, c], banks[h][:], r[:, c], ALU.mult)
+                nc.vector.scalar_tensor_tensor(r[:, c], r[:, c], -1.0, banks[h][:], ALU.add, ALU.mult)
+                nc.vector.tensor_tensor(r[:, c], r[:, c], wg[0][:, c], ALU.mult)
+                nc.vector.tensor_copy(page[0][:].indirect(idx2[:, 32 * h : 32 * (h + 1)]), r[:, c])
+            nc.sync.dma_start(rows_out1[0, 0], page[0][:])
+
+        def replace(i, lc, lw):
+            new = tile([P, S], F32, "new3", tag="woven1") if i == 3 else rt[i]
+            nc.vector.scalar_tensor_tensor(new[:], lc[:], -1.0, lw[:], ALU.add, ALU.mult)
+            nc.vector.tensor_copy(page[i][:].indirect(idx2[:]), new[:])
             nc.sync.dma_start(rows_out1[i // 4, i % 4], page[i][:])
 
         def round_plane(i):
-            g, t = i // 4, i % 4
-            w = widths[g]
-            if t == 0:
-                planes[g] = [
-                    tile([P, 4, w], BF16, "plane%d%d" % (g, c), tag=plane_tags[g][c]) for c in range(T2 // w)
-                ]
-            for c in range(T2 // w):
-                nc.scalar.copy(planes[g][c][:, t, :], page[i][:, w * c : w * (c + 1)])
+            if i == 0:
+                planes["first"] = [tile([P, 4, 1024], BF16, "first%d" % c, tag="tabw%d" % c) for c in range(2)]
+            if i == 4:
+                planes["low"] = [tile([P, 2, 1024], BF16, "low%d" % c, tag="right%d" % c) for c in range(2)]
+            if i == 6:
+                tags = ["right2", "right3", "w1c00", "w1c01"]
+                planes["high"] = [tile([P, 2, BANK], BF16, "high%d" % c, tag=tags[c]) for c in range(4)]
+            tiles, row = (planes["first"], i) if i < 4 else (planes["low" if i < 6 else "high"], i % 2)
+            w = T2 // len(tiles)
+            for c in range(len(tiles)):
+                nc.scalar.copy(tiles[c][:, row, :], page[i][:, w * c : w * (c + 1)])
 
-        def quant_page(g):
+        def quantize_page(g, c, woven):
             w = widths[g]
-            for c in range(T2 // w):
-                if g == 0:
-                    woven = tile([P, 4 * w], BF16, "woven%d" % c, tag="w1raw0%d" % c)
-                else:
-                    woven = ring.tile([P, 4 * w], BF16, name="woven", tag="bf", align_bytes=64)
-                dst = woven[:].rearrange("p (c i t) -> p c t i", i=4, t=4)
-                src = planes[g][c][:].rearrange("p t (c i) -> p c t i", i=4)
-                if g == 0:
-                    nc.scalar.copy(dst, src)
-                else:
-                    nc.vector.tensor_copy(dst, src)
-                cols = slice(w * c, w * (c + 1))
-                nc.vector.quantize_mx(out=codes[g][:, cols].bitcast(FP8X4), scales=scales[g][:, cols], in_=woven[:])
-                nc.sync.dma_start(
-                    out_2[g].rearrange("p m t -> p (m t)").bitcast(I32)[:, cols], codes[g][:, cols].bitcast(I32)
-                )
+            cols = slice(w * c, w * (c + 1))
+            words = tile([P, w], U32, "codes%d%d" % (g, c), tag=("right%d" % (4 + c) if g == 0 else None))
+            for b in range(w // BANK):
+                codes[g, c * w // BANK + b] = words[:, BANK * b : BANK * (b + 1)]
+            nc.vector.quantize_mx(out=words[:].bitcast(FP8X4), scales=scales[g][:, cols], in_=woven[:])
+            nc.sync.dma_start(out_2[g].rearrange("p m t -> p (m t)").bitcast(I32)[:, cols], words[:].bitcast(I32))
+
+        def store_scales(g):
             for q in range(4):
                 nc.sync.dma_start(
                     out_3[g, 4 * q : 4 * q + 4, :].bitcast(I32), scales[g][32 * q : 32 * q + 4, :].bitcast(I32)
                 )
 
-        made = {0: prepare(0), 1: prepare(1)}
-        for i in range(8):
-            replace(i, made[i])
-            if i == 0:
-                quant_w1(1, 0, False)
-                quant_w1(1, 1, False)
-            if i + 2 < 8:
-                made[i + 2] = prepare(i + 2)
-            round_plane(i)
-            if i == 5:
-                quant_page(0)
-        quant_page(1)
+        def quant_first_group():
+            for c in range(2):
+                woven = tile([P, 4 * widths[0]], BF16, "woven0%d" % c, tag="w1raw0%d" % c)
+                nc.scalar.copy(
+                    woven[:].rearrange("p (c i t) -> p c t i", i=4, t=4),
+                    planes["first"][c][:].rearrange("p t (c i) -> p c t i", i=4),
+                )
+                quantize_page(0, c, woven)
+            store_scales(0)
+
+        def weave_pair(engine_copy, woven, pair, t0):
+            engine_copy(
+                woven[:].rearrange("p (m t) -> p m t", t=4)[:, :, t0 : t0 + 2], pair.rearrange("p t m -> p m t")
+            )
+
+        replace_first()
+        lc = {i: copy_left(i) for i in range(1, 4)}
+        for i in range(1, 8):
+            if i == 3:
+                both = tile([P, 1024], U32, "w1c1", tag="right2")
+                w1c[1, 0], w1c[1, 1] = both[:, 0:512], both[:, 512:1024]
+                quant_w1(1, 0, 0, 4, "woven0", False)
+                quant_w1(1, 1, 0, 4, "woven1", False)
+                for j in range(4, 7):
+                    lc[j] = copy_left(j)
+            replace(i, lc[i], products(i, lc[i]))
+            if i == 3:
+                lc[7] = copy_left(7)
+            round_plane(i - 1)
+        quant_first_group()
+        last = [tile([P, 4 * BANK], BF16, "woven1%d" % c, tag="woven%d" % c) for c in range(4)]
+        for c in range(4):
+            weave_pair(nc.scalar.copy, last[c], planes["low"][c // 2][:, :, halves[c % 2]], 0)
+        round_plane(7)
+        for c in range(4):
+            weave_pair(nc.vector.tensor_copy, last[c], planes["high"][c][:], 2)
+            quantize_page(1, c, last[c])
+        store_scales(1)
 
         stage_tags = ["w1raw10", "w1raw11", "w1raw00", "w1raw01"]
         rows_out0 = out_0.rearrange("(n p) m -> p n m", p=P)
@@ -241,14 +267,17 @@ def tile_list_turf_probe_page_kernel(
                         out=acc[:],
                         lhsT=w2w[:, g, 2 * P * n : 2 * P * (n + 1)].bitcast(FP4X4),
                         lhsT_scale=w2s[:, g, P * n : P * (n + 1)],
-                        rhs=codes[g][:, cols].bitcast(FP8X4),
+                        rhs=codes[g, c].bitcast(FP8X4),
                         rhs_scale=scales[g][:, cols],
                         start=(g == 0),
                         stop=(g == 1),
                     )
                 y = staged[:, n, :]
-                if k < 4 or k % 3 == 1:
+                if k < 4 or k in (7, 11):
                     nc.scalar.activation(y, acc[:], ACT.Square)
+                elif k % 2 == 0:
+                    nc.vector.tensor_copy(y, acc[:])
+                    nc.gpsimd.tensor_tensor(y, y, y, ALU.mult)
                 else:
                     nc.vector.tensor_copy(y, acc[:])
                     nc.vector.tensor_tensor(y, acc[:], y, ALU.mult)

@@ -28,7 +28,7 @@ def tile_list_turf_probe_page_kernel(
     with ExitStack() as ctx:
         lists = ctx.enter_context(tc.tile_pool(name="lists", bufs=1))
         sb = ctx.enter_context(tc.tile_pool(name="sb", bufs=1))
-        ring = ctx.enter_context(tc.tile_pool(name="ring", bufs=4))
+        ring = ctx.enter_context(tc.tile_pool(name="ring", bufs=3))
         psum = ctx.enter_context(tc.psum_pool(name="psum", bufs=1))
 
         def tile(shape, dtype, name, tag=None):
@@ -51,7 +51,7 @@ def tile_list_turf_probe_page_kernel(
         rows_out1 = out_1.rearrange("(g p t) m -> g t p m", g=2, t=4)
         rows_wgs = wgs.rearrange("(q t) j -> q t j", t=4)
 
-        nc.vector.memset(tabs[:].bitcast(I32), 0)
+        nc.gpsimd.memset(tabs[:].bitcast(I32), 0)
         nc.vector.memset(w2s[:].rearrange("p a c -> p (a c)").bitcast(I32), 0)
         nc.vector.memset(warm[:], 1.0)
 
@@ -68,14 +68,14 @@ def tile_list_turf_probe_page_kernel(
         def load_page(i):
             nc.sync.dma_start(page[i][:], rows_page0[i // 4, i % 4])
 
-        def load_wg(t, cols=slice(0, S)):
+        def load_wg(t):
             for q in QUADS:
-                nc.sync.dma_start(wg[t][32 * q : 32 * (q + 1), cols], rows_wgs[:, t, cols])
+                nc.sync.dma_start(wg[t][32 * q : 32 * (q + 1), :], rows_wgs[:, t, :])
 
         load_tabw(0)
         nc.sync.dma_start(idx[:], offs)
         for q in range(4):
-            nc.scalar.dma_start(
+            nc.sync.dma_start(
                 tabs[32 * q : 32 * q + 8, :].bitcast(I32), tab_scales[:, 4 * q : 4 * q + 4, :].bitcast(I32)
             )
         nc.scalar.activation(warm[:], warm[:], ACT.Ln)
@@ -84,19 +84,18 @@ def tile_list_turf_probe_page_kernel(
         load_w1(0, 1)
         nc.sync.dma_start(idx2[:], offs2)
         load_right(0)
-        load_wg(0, slice(0, BANK))
+        load_wg(0)
         load_page(0)
-        load_wg(0, slice(BANK, S))
-        load_wg(1)
         load_right(1)
+        load_wg(1)
         load_page(1)
-        load_wg(2)
         load_right(2)
         load_w1(1, 0)
         load_w1(1, 1)
+        load_wg(2)
         load_page(2)
-        load_wg(3)
         load_right(3)
+        load_wg(3)
         load_page(3)
         for i in range(4, 8):
             load_right(i)
@@ -159,37 +158,39 @@ def tile_list_turf_probe_page_kernel(
 
         def copy_left(i):
             banks = left_tile(i)
-            lc = ring.tile([P, S], F32, name="lc", tag="lc", align_bytes=64)
-            for h in range(2):
-                nc.scalar.copy(lc[:, halves[h]], banks[h][:])
-            return lc
+            mixed = ring.tile([P, S], F32, name="mixed", tag="mixed", align_bytes=64)
+            plain = ring.tile([P, BANK], F32, name="plain", tag="plain", align_bytes=64)
+            nc.scalar.copy(mixed[:, halves[0]], banks[0][:])
+            nc.scalar.activation(mixed[:, halves[1]], banks[1][:], ACT.Square)
+            nc.scalar.copy(plain[:], banks[1][:])
+            return mixed, plain
 
-        def products(i, lc):
-            lw = tile([P, S], F32, "lw")
-            nc.gpsimd.tensor_tensor(lw[:], lc[:], wg[i % 4][:], ALU.mult)
-            nc.gpsimd.tensor_tensor(lc[:], lc[:], rt[i][:], ALU.mult)
-            return lw
+        def scatter(i):
+            nc.vector.tensor_copy(page[i][:].indirect(idx2[:]), rt[i][:])
+            nc.sync.dma_start(rows_out1[i // 4, i % 4], page[i][:])
 
         def replace_first():
             banks = left_tile(0)
-            r = rt[0]
+            u = tile([P, S], F32, "u")
             for h in range(2):
-                c = halves[h]
-                nc.vector.tensor_tensor(r[:, c], banks[h][:], r[:, c], ALU.mult)
-                nc.vector.scalar_tensor_tensor(r[:, c], r[:, c], -1.0, banks[h][:], ALU.add, ALU.mult)
-                nc.vector.tensor_tensor(r[:, c], r[:, c], wg[0][:, c], ALU.mult)
-                nc.vector.tensor_copy(page[0][:].indirect(idx2[:, 32 * h : 32 * (h + 1)]), r[:, c])
-            nc.sync.dma_start(rows_out1[0, 0], page[0][:])
+                nc.vector.tensor_tensor(u[:, halves[h]], banks[h][:], rt[0][:, halves[h]], ALU.mult)
+            for h in range(2):
+                nc.vector.scalar_tensor_tensor(u[:, halves[h]], u[:, halves[h]], -1.0, banks[h][:], ALU.add, ALU.mult)
+            nc.vector.tensor_tensor(rt[0][:], u[:], wg[0][:], ALU.mult)
+            scatter(0)
 
-        def replace(i, lc, lw):
-            new = tile([P, S], F32, "new3", tag="woven1") if i == 3 else rt[i]
-            nc.vector.scalar_tensor_tensor(new[:], lc[:], -1.0, lw[:], ALU.add, ALU.mult)
-            nc.vector.tensor_copy(page[i][:].indirect(idx2[:]), new[:])
-            nc.sync.dma_start(rows_out1[i // 4, i % 4], page[i][:])
+        def replace(i, mixed, plain):
+            lo, hi = halves
+            u = tile([P, S], F32, "u")
+            nc.gpsimd.tensor_tensor(u[:], mixed[:], rt[i][:], ALU.mult)
+            nc.gpsimd.tensor_tensor(mixed[:, hi], u[:, hi], plain[:], ALU.subtract)
+            nc.gpsimd.tensor_tensor(rt[i][:], mixed[:], wg[i % 4][:], ALU.mult)
+            nc.vector.scalar_tensor_tensor(rt[i][:, lo], u[:, lo], -1.0, rt[i][:, lo], ALU.add, ALU.mult)
+            scatter(i)
 
         def round_plane(i):
             if i == 0:
-                planes["first"] = [tile([P, 4, 1024], BF16, "first%d" % c, tag="tabw%d" % c) for c in range(2)]
+                planes["first"] = [tile([P, 4, 1024], BF16, "first%d" % c, tag="w1raw1%d" % c) for c in range(2)]
             if i == 4:
                 planes["low"] = [tile([P, 2, 1024], BF16, "low%d" % c, tag="right%d" % c) for c in range(2)]
             if i == 6:
@@ -198,7 +199,7 @@ def tile_list_turf_probe_page_kernel(
             tiles, row = (planes["first"], i) if i < 4 else (planes["low" if i < 6 else "high"], i % 2)
             w = T2 // len(tiles)
             for c in range(len(tiles)):
-                nc.scalar.copy(tiles[c][:, row, :], page[i][:, w * c : w * (c + 1)])
+                (nc.vector.tensor_copy if (i == 7 and c == 0) else nc.scalar.copy)(tiles[c][:, row, :], page[i][:, w * c : w * (c + 1)])
 
         def quantize_page(g, c, woven):
             w = widths[g]
@@ -231,18 +232,16 @@ def tile_list_turf_probe_page_kernel(
             )
 
         replace_first()
-        lc = {i: copy_left(i) for i in range(1, 4)}
+        left = {i: copy_left(i) for i in range(1, 4)}
         for i in range(1, 8):
-            if i == 3:
-                both = tile([P, 1024], U32, "w1c1", tag="right2")
+            replace(i, *left[i])
+            if i == 1:
+                both = tile([P, 1024], U32, "w1c1", tag="right1")
                 w1c[1, 0], w1c[1, 1] = both[:, 0:512], both[:, 512:1024]
                 quant_w1(1, 0, 0, 4, "woven0", False)
                 quant_w1(1, 1, 0, 4, "woven1", False)
-                for j in range(4, 7):
-                    lc[j] = copy_left(j)
-            replace(i, lc[i], products(i, lc[i]))
-            if i == 3:
-                lc[7] = copy_left(7)
+            if i + 3 < 8:
+                left[i + 3] = copy_left(i + 3)
             round_plane(i - 1)
         quant_first_group()
         last = [tile([P, 4 * BANK], BF16, "woven1%d" % c, tag="woven%d" % c) for c in range(4)]
@@ -273,7 +272,7 @@ def tile_list_turf_probe_page_kernel(
                         stop=(g == 1),
                     )
                 y = staged[:, n, :]
-                if k < 4 or k in (7, 11):
+                if k < 6:
                     nc.scalar.activation(y, acc[:], ACT.Square)
                 elif k % 2 == 0:
                     nc.vector.tensor_copy(y, acc[:])

@@ -19,6 +19,8 @@ ACT = mybir.ActivationFunctionType
 P = 128
 BANK = 512
 QUADS = (0, 2, 1, 3)
+SHARED = (1, 2, 3, 4, 5, 6, 7)
+CHUNKS = (256, 256, 512, 512, 512)
 
 
 def tile_list_turf_probe_page_kernel(
@@ -52,8 +54,9 @@ def tile_list_turf_probe_page_kernel(
         rows_wgs = wgs.rearrange("(q t) j -> q t j", t=4)
 
         nc.gpsimd.memset(tabs[:].bitcast(I32), 0)
-        nc.vector.memset(w2s[:].rearrange("p a c -> p (a c)").bitcast(I32), 0)
         nc.vector.memset(warm[:], 1.0)
+        nc.vector.memset(w2s[:].rearrange("p a c -> p (a c)").bitcast(I32), 0)
+        nc.scalar.activation(warm[:], warm[:], ACT.Ln)
 
         def load_tabw(a):
             nc.sync.dma_start(tabw[a][:].bitcast(I32), tab_words[a].rearrange("p t i -> p (t i)").bitcast(I32))
@@ -72,34 +75,33 @@ def tile_list_turf_probe_page_kernel(
             for q in QUADS:
                 nc.sync.dma_start(wg[t][32 * q : 32 * (q + 1), :], rows_wgs[:, t, :])
 
-        load_tabw(0)
         nc.sync.dma_start(idx[:], offs)
+        load_tabw(0)
         for q in range(4):
             nc.sync.dma_start(
                 tabs[32 * q : 32 * q + 8, :].bitcast(I32), tab_scales[:, 4 * q : 4 * q + 4, :].bitcast(I32)
             )
-        nc.scalar.activation(warm[:], warm[:], ACT.Ln)
         load_tabw(1)
         load_w1(0, 0)
         load_w1(0, 1)
-        nc.sync.dma_start(idx2[:], offs2)
         load_right(0)
         load_wg(0)
+        nc.sync.dma_start(idx2[:], offs2)
         load_page(0)
         load_right(1)
         load_wg(1)
-        load_page(1)
         load_right(2)
         load_w1(1, 0)
         load_w1(1, 1)
+        load_page(1)
         load_wg(2)
-        load_page(2)
         load_right(3)
+        load_page(2)
         load_wg(3)
-        load_page(3)
         for i in range(4, 8):
             load_right(i)
-            load_page(i)
+            load_page(i - 1)
+        load_page(7)
         nc.sync.dma_start(w2w[:].bitcast(I32), w2_words.rearrange("a p c -> p a c").bitcast(I32))
         for q in range(4):
             nc.sync.dma_start(
@@ -107,66 +109,73 @@ def tile_list_turf_probe_page_kernel(
                 w2_scales[:, 4 * q : 4 * q + 4, :].rearrange("a r c -> r a c").bitcast(I32),
             )
 
-        gs = tile([P, S], U8, "gs")
+        halves = [slice(0, BANK), slice(BANK, S)]
         gw = [tile([P, S], U32, "gw%d" % a) for a in range(2)]
+        gs = tile([P, S], U8, "gs")
         nc.vector.tensor_copy(gs[:], tabs[:].indirect(idx[:]))
-        w1c = {(0, a): tile([P, 512], U32, "w1c0%d" % a)[:] for a in range(2)}
-        w1s = [[tile([P, 512], U8, "w1s%d%d" % (g, a)) for a in range(2)] for g in range(2)]
+        for a in range(2):
+            nc.vector.tensor_copy(gw[a][:], tabw[a][:].indirect(idx[:]))
 
-        def quant_w1(g, a, t0, nt, tag, on_vector):
-            dealt = tile([P, 512 * nt], BF16, "w1bf", tag=tag)
-            dst = dealt[:].rearrange("p (t m j) -> p m j t", t=nt, j=4)
-            src = w1raw[g][a][:].rearrange("p j (m t) -> p m j t", t=4)[:, :, :, t0 : t0 + nt]
-            if on_vector:
-                nc.vector.tensor_copy(dst, src)
-            else:
-                nc.scalar.copy(dst, src)
-            cols = slice(P * t0, P * (t0 + nt))
-            nc.vector.quantize_mx(out=w1c[g, a][:, cols].bitcast(FP8X4), scales=w1s[g][a][:, cols], in_=dealt[:])
+        dealt = [tile([P, 2, 2, 1024], BF16, "dealt0", tag="woven1")]
+        w1c = [tile([P, 1024], U32, "w1c0")]
+        w1s = [tile([P, 1024], U8, "w1s%d" % g) for g in range(2)]
 
-        nc.vector.tensor_copy(gw[0][:], tabw[0][:].indirect(idx[:]))
-        nc.vector.tensor_copy(gw[1][:], tabw[1][:].indirect(idx[:]))
-        quant_w1(0, 0, 0, 2, "woven0", False)
-        quant_w1(0, 1, 0, 2, "woven1", True)
-        quant_w1(0, 0, 2, 2, "woven2", False)
-        quant_w1(0, 1, 2, 2, "woven3", False)
+        def deal(g, u, a, engine_copy=nc.scalar.copy):
+            dst = dealt[g][:, u, a, :].rearrange("p (t m j) -> p m j t", t=2, j=4)
+            src = w1raw[g][a][:].rearrange("p j (m t) -> p m j t", t=4)[:, :, :, 2 * u : 2 * u + 2]
+            engine_copy(dst, src)
 
-        codes = {}
-        scales = [tile([P, T2], U8, "scales%d" % g) for g in range(2)]
-        widths = [1024, 512]
-        planes = {}
+        def quant_w1(g, first, count):
+            cols = slice(256 * first, 256 * (first + count))
+            nc.vector.quantize_mx(
+                out=w1c[g][:, cols].bitcast(FP8X4),
+                scales=w1s[g][:, cols],
+                in_=dealt[g][:].rearrange("p u a c -> p (u a c)")[:, 1024 * first : 1024 * (first + count)],
+            )
+
+        deal(0, 0, 0)
+        quant_w1(0, 0, 1)
+        deal(0, 0, 1, nc.vector.tensor_copy)
+        quant_w1(0, 1, 1)
+        deal(0, 1, 0)
+        deal(0, 1, 1)
 
         def left_tile(i):
-            g, t = i // 4, i % 4
+            g, u, e = i // 4, (i % 4) // 2, i % 2
             banks = []
             for h in range(2):
-                acc = psum.tile([P, BANK], F32, name="left", tag="bank%d" % (2 * (i % 2) + h))
+                acc = psum.tile([P, BANK], F32, name="left", tag="bank%d" % (2 * (i % 4) + h))
                 for a in range(2):
+                    cols = slice(512 * u + 256 * a + P * e, 512 * u + 256 * a + P * (e + 1))
                     nc.tensor.matmul_mx(
                         out=acc[:],
-                        lhsT=w1c[g, a][:, P * t : P * (t + 1)].bitcast(FP8X4),
-                        lhsT_scale=w1s[g][a][:, P * t : P * (t + 1)],
-                        rhs=gw[a][:, BANK * h : BANK * (h + 1)].bitcast(FP8X4),
-                        rhs_scale=gs[4 * a : P, BANK * h : BANK * (h + 1)],
+                        lhsT=w1c[g][:, cols].bitcast(FP8X4),
+                        lhsT_scale=w1s[g][:, cols],
+                        rhs=gw[a][:, halves[h]].bitcast(FP8X4),
+                        rhs_scale=gs[4 * a : P, halves[h]],
                         start=(a == 0),
                         stop=(a == 1),
                     )
                 banks.append(acc)
             return banks
 
-        halves = [slice(0, BANK), slice(BANK, S)]
-
         def copy_left(i):
             banks = left_tile(i)
             mixed = ring.tile([P, S], F32, name="mixed", tag="mixed", align_bytes=64)
-            plain = ring.tile([P, BANK], F32, name="plain", tag="plain", align_bytes=64)
-            nc.scalar.copy(mixed[:, halves[0]], banks[0][:])
-            nc.scalar.activation(mixed[:, halves[1]], banks[1][:], ACT.Square)
-            nc.scalar.copy(plain[:], banks[1][:])
+            plain = ring.tile([P, S], F32, name="plain", tag="plain", align_bytes=64)
+            for h in range(2):
+                if i in SHARED and h == 0:
+                    nc.scalar.copy(mixed[:, halves[h]], banks[h][:])
+                else:
+                    nc.scalar.activation(mixed[:, halves[h]], banks[h][:], ACT.Square)
+                    nc.scalar.copy(plain[:, halves[h]], banks[h][:])
             return mixed, plain
 
+        def wg_rows(i):
+            return wg[i % 4][:]
+
         def scatter(i):
-            nc.vector.tensor_copy(page[i][:].indirect(idx2[:]), rt[i][:])
+            nc.vector.tensor_copy(page[i][:].indirect(idx2[:]), (first_values[0] if i == 0 else rt[i])[:])
             nc.sync.dma_start(rows_out1[i // 4, i % 4], page[i][:])
 
         def replace_first():
@@ -174,41 +183,49 @@ def tile_list_turf_probe_page_kernel(
             u = tile([P, S], F32, "u")
             for h in range(2):
                 nc.vector.tensor_tensor(u[:, halves[h]], banks[h][:], rt[0][:, halves[h]], ALU.mult)
-            for h in range(2):
                 nc.vector.scalar_tensor_tensor(u[:, halves[h]], u[:, halves[h]], -1.0, banks[h][:], ALU.add, ALU.mult)
-            nc.vector.tensor_tensor(rt[0][:], u[:], wg[0][:], ALU.mult)
-            scatter(0)
+            return u
 
         def replace(i, mixed, plain):
             lo, hi = halves
-            u = tile([P, S], F32, "u")
-            nc.gpsimd.tensor_tensor(u[:], mixed[:], rt[i][:], ALU.mult)
-            nc.gpsimd.tensor_tensor(mixed[:, hi], u[:, hi], plain[:], ALU.subtract)
-            nc.gpsimd.tensor_tensor(rt[i][:], mixed[:], wg[i % 4][:], ALU.mult)
-            nc.vector.scalar_tensor_tensor(rt[i][:, lo], u[:, lo], -1.0, rt[i][:, lo], ALU.add, ALU.mult)
-            scatter(i)
+            if i in SHARED:
+                u = tile([P, S], F32, "u")
+                nc.gpsimd.tensor_tensor(u[:], mixed[:], rt[i][:], ALU.mult)
+                nc.gpsimd.tensor_tensor(mixed[:, hi], u[:, hi], plain[:, hi], ALU.subtract)
+                nc.gpsimd.tensor_tensor(rt[i][:], mixed[:], wg_rows(i), ALU.mult)
+                nc.vector.scalar_tensor_tensor(rt[i][:, lo], u[:, lo], -1.0, rt[i][:, lo], ALU.add, ALU.mult)
+            else:
+                u = tile([P, S], F32, "u")
+                nc.gpsimd.tensor_tensor(u[:], mixed[:], rt[i][:], ALU.mult)
+                nc.gpsimd.tensor_tensor(u[:], u[:], plain[:], ALU.subtract)
+                nc.gpsimd.tensor_tensor(rt[i][:], u[:], wg_rows(i), ALU.mult)
 
-        def round_plane(i):
-            if i == 0:
-                planes["first"] = [tile([P, 4, 1024], BF16, "first%d" % c, tag="w1raw1%d" % c) for c in range(2)]
-            if i == 4:
-                planes["low"] = [tile([P, 2, 1024], BF16, "low%d" % c, tag="right%d" % c) for c in range(2)]
-            if i == 6:
-                tags = ["right2", "right3", "w1c00", "w1c01"]
-                planes["high"] = [tile([P, 2, BANK], BF16, "high%d" % c, tag=tags[c]) for c in range(4)]
-            tiles, row = (planes["first"], i) if i < 4 else (planes["low" if i < 6 else "high"], i % 2)
-            w = T2 // len(tiles)
-            for c in range(len(tiles)):
-                (nc.vector.tensor_copy if (i == 7 and c == 0) else nc.scalar.copy)(tiles[c][:, row, :], page[i][:, w * c : w * (c + 1)])
+        plane_tags = [["w1raw10", "w1raw11"], ["w1raw00", "w1raw01"]]
+        planes = {}
 
-        def quantize_page(g, c, woven):
-            w = widths[g]
-            cols = slice(w * c, w * (c + 1))
-            words = tile([P, w], U32, "codes%d%d" % (g, c), tag=("right%d" % (4 + c) if g == 0 else None))
-            for b in range(w // BANK):
-                codes[g, c * w // BANK + b] = words[:, BANK * b : BANK * (b + 1)]
-            nc.vector.quantize_mx(out=words[:].bitcast(FP8X4), scales=scales[g][:, cols], in_=woven[:])
-            nc.sync.dma_start(out_2[g].rearrange("p m t -> p (m t)").bitcast(I32)[:, cols], words[:].bitcast(I32))
+        def round_plane(i, cols, engine_copy):
+            g, c = i // 4, cols.start // 1024
+            if (g, c) not in planes:
+                planes[g, c] = tile([P, 4, 1024], BF16, "planes%d%d" % (g, c), tag=plane_tags[g][c])
+            engine_copy(planes[g, c][:, i % 4, cols.start - 1024 * c : cols.stop - 1024 * c], page[i][:, cols])
+
+        def round_page(i):
+            for c in range(2):
+                round_plane(i, slice(1024 * c, 1024 * (c + 1)), nc.scalar.copy)
+
+        def weave(engine_copy, woven, g, cols):
+            c = cols.start // 1024
+            engine_copy(
+                woven.rearrange("p (c i t) -> p c t i", i=4, t=4),
+                planes[g, c][:, :, cols.start - 1024 * c : cols.stop - 1024 * c].rearrange("p t (c i) -> p c t i", i=4),
+            )
+
+        codes = {}
+        scales = [tile([P, T2], U8, "scales%d" % g) for g in range(2)]
+
+        def quantize_page(g, cols, woven, words):
+            nc.vector.quantize_mx(out=words.bitcast(FP8X4), scales=scales[g][:, cols], in_=woven)
+            nc.sync.dma_start(out_2[g].rearrange("p m t -> p (m t)").bitcast(I32)[:, cols], words.bitcast(I32))
 
         def store_scales(g):
             for q in range(4):
@@ -216,72 +233,92 @@ def tile_list_turf_probe_page_kernel(
                     out_3[g, 4 * q : 4 * q + 4, :].bitcast(I32), scales[g][32 * q : 32 * q + 4, :].bitcast(I32)
                 )
 
-        def quant_first_group():
-            for c in range(2):
-                woven = tile([P, 4 * widths[0]], BF16, "woven0%d" % c, tag="w1raw0%d" % c)
-                nc.scalar.copy(
-                    woven[:].rearrange("p (c i t) -> p c t i", i=4, t=4),
-                    planes["first"][c][:].rearrange("p t (c i) -> p c t i", i=4),
-                )
-                quantize_page(0, c, woven)
-            store_scales(0)
-
-        def weave_pair(engine_copy, woven, pair, t0):
-            engine_copy(
-                woven[:].rearrange("p (m t) -> p m t", t=4)[:, :, t0 : t0 + 2], pair.rearrange("p t m -> p m t")
-            )
-
-        replace_first()
-        left = {i: copy_left(i) for i in range(1, 4)}
+        u_first = replace_first()
+        left = {1: copy_left(1)}
+        quant_w1(0, 2, 2)
+        first_values = [tile([P, S], F32, "first_values", tag="woven1")]
+        nc.vector.tensor_tensor(first_values[0][:], u_first[:], wg_rows(0), ALU.mult)
+        scatter(0)
+        left[2] = copy_left(2)
+        left[3] = copy_left(3)
+        dealt.append(tile([P, 2, 2, 1024], BF16, "dealt1", tag="woven1"))
+        for a in range(2):
+            for u in range(2):
+                deal(1, u, a)
         for i in range(1, 8):
             replace(i, *left[i])
+            if i == 7:
+                codes[0] = tile([P, T2], U32, "codes0", tag="right6")
+                for c in range(2):
+                    quantize_page(0, slice(1024 * c, 1024 * (c + 1)), first[c][:], codes[0][:, 1024 * c : 1024 * (c + 1)])
+                store_scales(0)
+            scatter(i)
             if i == 1:
-                both = tile([P, 1024], U32, "w1c1", tag="right1")
-                w1c[1, 0], w1c[1, 1] = both[:, 0:512], both[:, 512:1024]
-                quant_w1(1, 0, 0, 4, "woven0", False)
-                quant_w1(1, 1, 0, 4, "woven1", False)
+                w1c.append(tile([P, 1024], U32, "w1c1", tag="right1"))
+                quant_w1(1, 0, 4)
             if i + 3 < 8:
                 left[i + 3] = copy_left(i + 3)
-            round_plane(i - 1)
-        quant_first_group()
-        last = [tile([P, 4 * BANK], BF16, "woven1%d" % c, tag="woven%d" % c) for c in range(4)]
-        for c in range(4):
-            weave_pair(nc.scalar.copy, last[c], planes["low"][c // 2][:, :, halves[c % 2]], 0)
-        round_plane(7)
-        for c in range(4):
-            weave_pair(nc.vector.tensor_copy, last[c], planes["high"][c][:], 2)
-            quantize_page(1, c, last[c])
+            round_page(i - 1)
+            if i == 4:
+                first = [tile([P, 4096], BF16, "woven0%d" % c, tag="tabw%d" % c) for c in range(2)]
+                for b in range(4):
+                    weave(nc.scalar.copy, first[b // 2][:, 2048 * (b % 2) : 2048 * (b % 2 + 1)], 0, slice(BANK * b, BANK * (b + 1)))
+
+        edges = [sum(CHUNKS[:c]) for c in range(len(CHUNKS) + 1)]
+        chunks = [slice(edges[c], edges[c + 1]) for c in range(len(CHUNKS))]
+        accs = {}
+
+        def product(k, g):
+            c, n = k // 4, k % 4
+            if g == 0:
+                accs[k] = psum.tile([P, BANK], F32, name="prod", tag="bank%d" % (k % 8))[:, 0 : CHUNKS[c]]
+            nc.tensor.matmul_mx(
+                out=accs[k],
+                lhsT=w2w[:, g, 2 * P * n : 2 * P * (n + 1)].bitcast(FP4X4),
+                lhsT_scale=w2s[:, g, P * n : P * (n + 1)],
+                rhs=(codes[0][:, chunks[c]] if g == 0 else last_codes[c][:]).bitcast(FP8X4),
+                rhs_scale=scales[g][:, chunks[c]],
+                start=(g == 0),
+                stop=(g == 1),
+            )
+
+        for k in range(8):
+            product(k, 0)
+
+        woven_tags = ["right2", "right3", "right4", "right5", "woven1"]
+        code_tags = ["gw0", "gw1", "w1c0", "right0", "right1"]
+        last = [tile([P, 4 * w], BF16, "woven1%d" % c, tag=woven_tags[c]) for c, w in enumerate(CHUNKS)]
+        last_codes = [tile([P, w], U32, "codes1%d" % c, tag=code_tags[c]) for c, w in enumerate(CHUNKS)]
+        for c in range(len(CHUNKS)):
+            round_plane(7, chunks[c], nc.vector.tensor_copy if c < 2 else nc.scalar.copy)
+        for c, cols in enumerate(chunks):
+            weave(nc.vector.tensor_copy, last[c][:], 1, cols)
+            quantize_page(1, cols, last[c][:], last_codes[c][:])
         store_scales(1)
 
-        stage_tags = ["w1raw10", "w1raw11", "w1raw00", "w1raw01"]
         rows_out0 = out_0.rearrange("(n p) m -> p n m", p=P)
-        for c in range(4):
-            cols = slice(BANK * c, BANK * (c + 1))
-            staged = tile([P, 4, BANK], F32, "staged%d" % c, tag=stage_tags[c])
-            for n in range(4):
-                k = 4 * c + n
-                acc = psum.tile([P, BANK], F32, name="prod", tag="bank%d" % ((k + 4) % 8))
-                for g in range(2):
-                    nc.tensor.matmul_mx(
-                        out=acc[:],
-                        lhsT=w2w[:, g, 2 * P * n : 2 * P * (n + 1)].bitcast(FP4X4),
-                        lhsT_scale=w2s[:, g, P * n : P * (n + 1)],
-                        rhs=codes[g, c].bitcast(FP8X4),
-                        rhs_scale=scales[g][:, cols],
-                        start=(g == 0),
-                        stop=(g == 1),
-                    )
-                y = staged[:, n, :]
-                if k < 6:
-                    nc.scalar.activation(y, acc[:], ACT.Square)
-                elif k % 2 == 0:
-                    nc.vector.tensor_copy(y, acc[:])
-                    nc.gpsimd.tensor_tensor(y, y, y, ALU.mult)
-                else:
-                    nc.vector.tensor_copy(y, acc[:])
-                    nc.vector.tensor_tensor(y, acc[:], y, ALU.mult)
-                nc.scalar.activation(y, y, ACT.Ln, bias=1.0)
-                if c == 3:
-                    nc.sync.dma_start(rows_out0[:, n, cols], y)
-                elif n % 2 == 1:
-                    nc.sync.dma_start(rows_out0[:, n - 1 : n + 1, cols], staged[:, n - 1 : n + 1, :])
+        early = tile([P, 2, 4, 256], F32, "staged_early", tag="w1raw10")
+        middle = tile([P, 4, BANK], F32, "staged_middle", tag="w1raw11")
+        late = tile([P, 2, 4, BANK], F32, "staged_late", tag="woven1")
+        staged = [early[:, 0], early[:, 1], middle[:], late[:, 0], late[:, 1]]
+        roles = "SSSSSSSSSSSVGGGGGVVV"
+        for k in range(4 * len(CHUNKS)):
+            c, n = k // 4, k % 4
+            if k >= 8:
+                product(k, 0)
+            product(k, 1)
+            y = staged[c][:, n, :]
+            acc = accs[k]
+            if roles[k] == "S":
+                nc.scalar.activation(y, acc, ACT.Square)
+            elif roles[k] == "G":
+                nc.vector.tensor_copy(y, acc)
+                nc.gpsimd.tensor_tensor(y, y, y, ALU.mult)
+            else:
+                nc.vector.tensor_copy(y, acc)
+                nc.vector.tensor_tensor(y, acc, y, ALU.mult)
+            nc.scalar.activation(y, y, ACT.Ln, bias=1.0)
+            per_store = 4 if c < 2 else (2 if c < 4 else 1)
+            if (n + 1) % per_store == 0:
+                rows = slice(n + 1 - per_store, n + 1)
+                nc.sync.dma_start(rows_out0[:, rows, chunks[c]], staged[c][:, rows, :])

@@ -53,7 +53,7 @@ def tile_list_turf_probe_page_kernel(
         rows_out1 = out_1.rearrange("(g p t) m -> g t p m", g=2, t=4)
         rows_wgs = wgs.rearrange("(q t) j -> q t j", t=4)
 
-        nc.gpsimd.memset(tabs[:].bitcast(I32), 0)
+        nc.vector.memset(tabs[:].bitcast(I32), 0)
         nc.vector.memset(warm[:], 1.0)
         nc.vector.memset(w2s[:].rearrange("p a c -> p (a c)").bitcast(I32), 0)
         nc.scalar.activation(warm[:], warm[:], ACT.Ln)
@@ -77,11 +77,11 @@ def tile_list_turf_probe_page_kernel(
 
         nc.sync.dma_start(idx[:], offs)
         load_tabw(0)
+        load_tabw(1)
         for q in range(4):
             nc.sync.dma_start(
                 tabs[32 * q : 32 * q + 8, :].bitcast(I32), tab_scales[:, 4 * q : 4 * q + 4, :].bitcast(I32)
             )
-        load_tabw(1)
         load_w1(0, 0)
         load_w1(0, 1)
         load_right(0)
@@ -111,10 +111,10 @@ def tile_list_turf_probe_page_kernel(
 
         halves = [slice(0, BANK), slice(BANK, S)]
         gw = [tile([P, S], U32, "gw%d" % a) for a in range(2)]
-        gs = tile([P, S], U8, "gs")
-        nc.vector.tensor_copy(gs[:], tabs[:].indirect(idx[:]))
         for a in range(2):
             nc.vector.tensor_copy(gw[a][:], tabw[a][:].indirect(idx[:]))
+        gs = tile([P, S], U8, "gs", tag="tabw0")
+        nc.vector.tensor_copy(gs[:], tabs[:].indirect(idx[:]))
 
         dealt = [tile([P, 2, 2, 1024], BF16, "dealt0", tag="woven1")]
         w1c = [tile([P, 1024], U32, "w1c0")]
@@ -301,7 +301,7 @@ def tile_list_turf_probe_page_kernel(
         middle = tile([P, 4, BANK], F32, "staged_middle", tag="w1raw11")
         late = tile([P, 2, 4, BANK], F32, "staged_late", tag="woven1")
         staged = [early[:, 0], early[:, 1], middle[:], late[:, 0], late[:, 1]]
-        roles = "SSSSSSSSSSSVGGGGGVVV"
+        roles = "SSSSSSSSSSSSGGGGGVVV"
         for k in range(4 * len(CHUNKS)):
             c, n = k // 4, k % 4
             if k >= 8:

@@ -79,7 +79,7 @@ def tile_list_turf_probe_page_kernel(
         load_tabw(0)
         load_tabw(1)
         for q in range(4):
-            nc.sync.dma_start(
+            nc.gpsimd.dma_start(
                 tabs[32 * q : 32 * q + 8, :].bitcast(I32), tab_scales[:, 4 * q : 4 * q + 4, :].bitcast(I32)
             )
         load_w1(0, 0)

@@ -1,6 +1,7 @@
 from contextlib import ExitStack
 
 import concourse.mybir as mybir
+from concourse.masks import make_identity
 
 K, H, N, T, S, T2 = 1024, 1024, 512, 2048, 1024, 2048
 FLOPS = 2 * K * H * S + 2 * H * N * T2
@@ -18,8 +19,6 @@ ACT = mybir.ActivationFunctionType
 
 P = 128
 BANK = 512
-QUADS = (0, 2, 1, 3)
-SHARED = (1, 2, 3, 4, 5, 6, 7)
 CHUNKS = (256, 256, 512, 512, 512)
 
 
@@ -47,11 +46,12 @@ def tile_list_turf_probe_page_kernel(
         w2w = tile([P, 2, 2 * N], U8, "w2w")
         w2s = tile([P, 2, N], U8, "w2s")
         warm = tile([P, 1], F32, "warm")
+        ident = tile([P, P], F32, "ident")
+        wg_plain = tile([P, S], F32, "wg_plain", tag="u")
 
         rows_right = right.rearrange("(g p t) j -> g t p j", g=2, t=4)
         rows_page0 = page0.rearrange("(g p t) m -> g t p m", g=2, t=4)
         rows_out1 = out_1.rearrange("(g p t) m -> g t p m", g=2, t=4)
-        rows_wgs = wgs.rearrange("(q t) j -> q t j", t=4)
 
         nc.vector.memset(tabs[:].bitcast(I32), 0)
         nc.vector.memset(warm[:], 1.0)
@@ -71,45 +71,57 @@ def tile_list_turf_probe_page_kernel(
         def load_page(i):
             nc.sync.dma_start(page[i][:], rows_page0[i // 4, i % 4])
 
-        def load_wg(t):
-            for q in QUADS:
-                nc.sync.dma_start(wg[t][32 * q : 32 * (q + 1), :], rows_wgs[:, t, :])
-
         nc.sync.dma_start(idx[:], offs)
         load_tabw(0)
+        nc.sync.dma_start(wg_plain[:], wgs)
         load_tabw(1)
         for q in range(4):
             nc.gpsimd.dma_start(
                 tabs[32 * q : 32 * q + 8, :].bitcast(I32), tab_scales[:, 4 * q : 4 * q + 4, :].bitcast(I32)
             )
+        make_identity(nc, ident[:])
         load_w1(0, 0)
         load_w1(0, 1)
         load_right(0)
-        load_wg(0)
         nc.sync.dma_start(idx2[:], offs2)
         load_page(0)
         load_right(1)
-        load_wg(1)
         load_right(2)
+        load_page(1)
         load_w1(1, 0)
         load_w1(1, 1)
-        load_page(1)
-        load_wg(2)
-        load_right(3)
-        load_page(2)
-        load_wg(3)
-        for i in range(4, 8):
+        for i in range(3, 8):
             load_right(i)
             load_page(i - 1)
         load_page(7)
         nc.sync.dma_start(w2w[:].bitcast(I32), w2_words.rearrange("a p c -> p a c").bitcast(I32))
         for q in range(4):
-            nc.sync.dma_start(
+            nc.gpsimd.dma_start(
                 w2s[32 * q : 32 * q + 4, :, :].bitcast(I32),
                 w2_scales[:, 4 * q : 4 * q + 4, :].rearrange("a r c -> r a c").bitcast(I32),
             )
 
         halves = [slice(0, BANK), slice(BANK, S)]
+        turned = [psum.tile([P, 4, P], F32, name="turned", tag="bank%d" % (6 + h)) for h in range(2)]
+        for c in range(8):
+            nc.tensor.transpose(turned[c // 4][:, c % 4, :], wg_plain[:, P * c : P * (c + 1)], ident[:])
+
+        def spread_wg(t):
+            spread = tile([P, 8, 4, 32], F32, "spread", tag="spread%d" % (t % 2))
+            for h in range(2):
+                rows = turned[h][:].rearrange("p c (q t) -> p c t q", t=4)[:, :, t : t + 1, :]
+                nc.scalar.copy(spread[:, 4 * h : 4 * (h + 1)], rows.to_broadcast([P, 4, 4, 32]))
+            return spread
+
+        def turn_wg(t, spread):
+            for h in range(2):
+                back = psum.tile([P, 4, P], F32, name="back", tag="bank%d" % (4 + h))
+                for c in range(4):
+                    nc.tensor.transpose(back[:, c, :], spread[:, 4 * h + c].rearrange("p a q -> p (a q)"), ident[:])
+                nc.scalar.copy(wg[t][:, halves[h]], back[:].rearrange("p c j -> p (c j)"))
+
+        spreads = [spread_wg(0), spread_wg(1)]
+        turn_wg(0, spreads[0])
         gw = [tile([P, S], U32, "gw%d" % a) for a in range(2)]
         for a in range(2):
             nc.vector.tensor_copy(gw[a][:], tabw[a][:].indirect(idx[:]))
@@ -139,13 +151,14 @@ def tile_list_turf_probe_page_kernel(
         quant_w1(0, 1, 1)
         deal(0, 1, 0)
         deal(0, 1, 1)
+        turn_wg(1, spreads[1])
 
         def left_tile(i):
             g, u, e = i // 4, (i % 4) // 2, i % 2
-            banks = []
-            for h in range(2):
-                acc = psum.tile([P, BANK], F32, name="left", tag="bank%d" % (2 * (i % 4) + h))
-                for a in range(2):
+            banks = [psum.tile([P, BANK], F32, name="left", tag="bank%d" % (2 * (i % 2) + h)) for h in range(2)]
+            for a in range(2):
+                for h in range(2):
+                    acc = banks[h]
                     cols = slice(512 * u + 256 * a + P * e, 512 * u + 256 * a + P * (e + 1))
                     nc.tensor.matmul_mx(
                         out=acc[:],
@@ -156,19 +169,15 @@ def tile_list_turf_probe_page_kernel(
                         start=(a == 0),
                         stop=(a == 1),
                     )
-                banks.append(acc)
             return banks
 
         def copy_left(i):
             banks = left_tile(i)
             mixed = ring.tile([P, S], F32, name="mixed", tag="mixed", align_bytes=64)
-            plain = ring.tile([P, S], F32, name="plain", tag="plain", align_bytes=64)
-            for h in range(2):
-                if i in SHARED and h == 0:
-                    nc.scalar.copy(mixed[:, halves[h]], banks[h][:])
-                else:
-                    nc.scalar.activation(mixed[:, halves[h]], banks[h][:], ACT.Square)
-                    nc.scalar.copy(plain[:, halves[h]], banks[h][:])
+            plain = ring.tile([P, BANK], F32, name="plain", tag="plain", align_bytes=64)
+            nc.scalar.copy(mixed[:, halves[0]], banks[0][:])
+            nc.scalar.activation(mixed[:, halves[1]], banks[1][:], ACT.Square)
+            nc.scalar.copy(plain[:], banks[1][:])
             return mixed, plain
 
         def wg_rows(i):
@@ -183,24 +192,19 @@ def tile_list_turf_probe_page_kernel(
             u = tile([P, S], F32, "u")
             for h in range(2):
                 nc.vector.tensor_tensor(u[:, halves[h]], banks[h][:], rt[0][:, halves[h]], ALU.mult)
+            for h in range(2):
                 nc.vector.scalar_tensor_tensor(u[:, halves[h]], u[:, halves[h]], -1.0, banks[h][:], ALU.add, ALU.mult)
             return u
 
         def replace(i, mixed, plain):
             lo, hi = halves
-            if i in SHARED:
-                u = tile([P, S], F32, "u")
-                nc.gpsimd.tensor_tensor(u[:], mixed[:], rt[i][:], ALU.mult)
-                nc.gpsimd.tensor_tensor(mixed[:, hi], u[:, hi], plain[:, hi], ALU.subtract)
-                nc.gpsimd.tensor_tensor(rt[i][:], mixed[:], wg_rows(i), ALU.mult)
-                nc.vector.scalar_tensor_tensor(rt[i][:, lo], u[:, lo], -1.0, rt[i][:, lo], ALU.add, ALU.mult)
-            else:
-                u = tile([P, S], F32, "u")
-                nc.gpsimd.tensor_tensor(u[:], mixed[:], rt[i][:], ALU.mult)
-                nc.gpsimd.tensor_tensor(u[:], u[:], plain[:], ALU.subtract)
-                nc.gpsimd.tensor_tensor(rt[i][:], u[:], wg_rows(i), ALU.mult)
+            u = tile([P, S], F32, "u")
+            nc.gpsimd.tensor_tensor(u[:], mixed[:], rt[i][:], ALU.mult)
+            nc.gpsimd.tensor_tensor(mixed[:, hi], u[:, hi], plain[:], ALU.subtract)
+            nc.gpsimd.tensor_tensor(rt[i][:], mixed[:], wg_rows(i), ALU.mult)
+            nc.vector.scalar_tensor_tensor(rt[i][:, lo], u[:, lo], -1.0, rt[i][:, lo], ALU.add, ALU.mult)
 
-        plane_tags = [["w1raw10", "w1raw11"], ["w1raw00", "w1raw01"]]
+        plane_tags = [["w1raw11", "woven1"], ["w1raw00", "w1raw01"]]
         planes = {}
 
         def round_plane(i, cols, engine_copy):
@@ -237,10 +241,13 @@ def tile_list_turf_probe_page_kernel(
         left = {1: copy_left(1)}
         quant_w1(0, 2, 2)
         first_values = [tile([P, S], F32, "first_values", tag="woven1")]
-        nc.vector.tensor_tensor(first_values[0][:], u_first[:], wg_rows(0), ALU.mult)
+        for h in range(2):
+            nc.vector.tensor_tensor(first_values[0][:, halves[h]], u_first[:, halves[h]], wg[0][:, halves[h]], ALU.mult)
         scatter(0)
         left[2] = copy_left(2)
+        turn_wg(2, spread_wg(2))
         left[3] = copy_left(3)
+        turn_wg(3, spread_wg(3))
         dealt.append(tile([P, 2, 2, 1024], BF16, "dealt1", tag="woven1"))
         for a in range(2):
             for u in range(2):

@@ -19,7 +19,14 @@ ACT = mybir.ActivationFunctionType
 
 P = 128
 BANK = 512
+SHARED = {1: "square0", 4: "right2"}
+WORK_TAGS = {1: "u", 2: "w1head11", 3: "w1head00", 4: "w1head00", 5: "w1c0", 6: "w1c0", 7: "w1c0"}
+SQUARE_TAGS = {1: "w1head11", 4: "w1c0", 7: "woven1"}
 CHUNKS = (256, 256, 512, 512, 512)
+ROLES = "SSSSSSSSGGGVGVVV"
+SQUARE_ORDER = range(8, 16)
+FINISH_ORDER = (8, 9, 11, 10, 13, 12, 14, 15)
+STORES = {2: (0, 2), 3: (2, 4), 4: (0, 1), 5: (1, 2), 6: (2, 3), 7: (3, 4), 8: (0, 1), 9: (1, 2), 10: (2, 3), 11: (3, 4), 12: (0, 1), 13: (1, 2), 14: (2, 3), 15: (3, 4)}
 
 
 def tile_list_turf_probe_page_kernel(
@@ -39,19 +46,21 @@ def tile_list_turf_probe_page_kernel(
         idx2 = lists.tile([P, S // 16], U16, name="idx2")
         tabw = [tile([P, T], U32, "tabw%d" % a) for a in range(2)]
         tabs = tile([P, T], U8, "tabs")
-        w1raw = [[tile([P, 4, 512], F32, "w1raw%d%d" % (g, a)) for a in range(2)] for g in range(2)]
-        rt = [tile([P, S], F32, "right%d" % i) for i in range(8)]
+        w1head = {(u, a): tile([P, 4, 256], F32, "w1head%d%d" % (u, a)) for u in range(2) for a in range(2)}
+        w1raw = [tile([P, 4, 512], F32, "w1raw1%d" % a) for a in range(2)]
+        rt = [tile([P, S], F32, "right%d" % i) for i in range(6)]
         wg = [tile([P, S], F32, "wg%d" % t) for t in range(4)]
         page = [tile([P, T2], F32, "page%d" % i) for i in range(8)]
-        w2w = tile([P, 2, 2 * N], U8, "w2w")
         w2s = tile([P, 2, N], U8, "w2s")
         warm = tile([P, 1], F32, "warm")
         ident = tile([P, P], F32, "ident")
-        wg_plain = tile([P, S], F32, "wg_plain", tag="u")
+        ident_bf = tile([P, P], BF16, "ident_bf")
+        wg_plain = tile([P, S], F32, "wg_plain")
 
-        rows_right = right.rearrange("(g p t) j -> g t p j", g=2, t=4)
-        rows_page0 = page0.rearrange("(g p t) m -> g t p m", g=2, t=4)
-        rows_out1 = out_1.rearrange("(g p t) m -> g t p m", g=2, t=4)
+        def rows(matrix, i):
+            if i < 4:
+                return matrix[P * i : P * (i + 1), :]
+            return matrix[512:1024, :].rearrange("(p t) m -> t p m", t=4)[i - 4]
 
         nc.vector.memset(tabs[:].bitcast(I32), 0)
         nc.vector.memset(warm[:], 1.0)
@@ -61,53 +70,48 @@ def tile_list_turf_probe_page_kernel(
         def load_tabw(a):
             nc.sync.dma_start(tabw[a][:].bitcast(I32), tab_words[a].rearrange("p t i -> p (t i)").bitcast(I32))
 
-        def load_w1(g, a):
-            src = w1[512 * a : 512 * (a + 1), 512 * g : 512 * (g + 1)].rearrange("(p j) c -> p j c", j=4)
-            nc.sync.dma_start(w1raw[g][a][:], src)
+        def load_w1(dst, a, cols):
+            nc.sync.dma_start(dst[:], w1[512 * a : 512 * (a + 1), cols].rearrange("(p j) c -> p j c", j=4))
 
         def load_right(i):
-            nc.sync.dma_start(rt[i][:], rows_right[i // 4, i % 4])
+            nc.sync.dma_start(rt[i][:], rows(right, i))
 
         def load_page(i):
-            nc.sync.dma_start(page[i][:], rows_page0[i // 4, i % 4])
+            nc.sync.dma_start(page[i][:], rows(page0, i))
 
-        nc.sync.dma_start(idx[:], offs)
         load_tabw(0)
-        nc.sync.dma_start(wg_plain[:], wgs)
+        nc.sync.dma_start(idx[:], offs)
         load_tabw(1)
         for q in range(4):
             nc.gpsimd.dma_start(
                 tabs[32 * q : 32 * q + 8, :].bitcast(I32), tab_scales[:, 4 * q : 4 * q + 4, :].bitcast(I32)
             )
         make_identity(nc, ident[:])
-        load_w1(0, 0)
-        load_w1(0, 1)
+        make_identity(nc, ident_bf[:])
+        for a in range(2):
+            load_w1(w1head[0, a], a, slice(0, 256))
         load_right(0)
+        nc.sync.dma_start(rt[1][:, 0:BANK], rows(right, 1)[:, 0:BANK])
+        for a in range(2):
+            load_w1(w1head[1, a], a, slice(256, 512))
+        nc.sync.dma_start(wg_plain[:], wgs)
         nc.sync.dma_start(idx2[:], offs2)
         load_page(0)
-        load_right(1)
+        nc.sync.dma_start(rt[1][:, BANK:S], rows(right, 1)[:, BANK:S])
         load_right(2)
         load_page(1)
-        load_w1(1, 0)
-        load_w1(1, 1)
-        for i in range(3, 8):
+        for a in range(2):
+            load_w1(w1raw[a], a, slice(512, 1024))
+        for i in range(3, 6):
             load_right(i)
             load_page(i - 1)
-        load_page(7)
-        nc.sync.dma_start(w2w[:].bitcast(I32), w2_words.rearrange("a p c -> p a c").bitcast(I32))
-        for q in range(4):
-            nc.gpsimd.dma_start(
-                w2s[32 * q : 32 * q + 4, :, :].bitcast(I32),
-                w2_scales[:, 4 * q : 4 * q + 4, :].rearrange("a r c -> r a c").bitcast(I32),
-            )
+        load_page(5)
 
         halves = [slice(0, BANK), slice(BANK, S)]
         turned = [psum.tile([P, 4, P], F32, name="turned", tag="bank%d" % (6 + h)) for h in range(2)]
-        for c in range(8):
-            nc.tensor.transpose(turned[c // 4][:, c % 4, :], wg_plain[:, P * c : P * (c + 1)], ident[:])
 
         def spread_wg(t):
-            spread = tile([P, 8, 4, 32], F32, "spread", tag="spread%d" % (t % 2))
+            spread = tile([P, 8, 4, 32], F32, "spread", tag="right%d" % (6 + t % 2))
             for h in range(2):
                 rows = turned[h][:].rearrange("p c (q t) -> p c t q", t=4)[:, :, t : t + 1, :]
                 nc.scalar.copy(spread[:, 4 * h : 4 * (h + 1)], rows.to_broadcast([P, 4, 4, 32]))
@@ -120,109 +124,145 @@ def tile_list_turf_probe_page_kernel(
                     nc.tensor.transpose(back[:, c, :], spread[:, 4 * h + c].rearrange("p a q -> p (a q)"), ident[:])
                 nc.scalar.copy(wg[t][:, halves[h]], back[:].rearrange("p c j -> p (c j)"))
 
-        spreads = [spread_wg(0), spread_wg(1)]
-        turn_wg(0, spreads[0])
         gw = [tile([P, S], U32, "gw%d" % a) for a in range(2)]
         for a in range(2):
             nc.vector.tensor_copy(gw[a][:], tabw[a][:].indirect(idx[:]))
-        gs = tile([P, S], U8, "gs", tag="tabw0")
-        nc.vector.tensor_copy(gs[:], tabs[:].indirect(idx[:]))
+        gs = {}
 
-        dealt = [tile([P, 2, 2, 1024], BF16, "dealt0", tag="woven1")]
+        def gather_scales(h):
+            gs[h] = tile([P, BANK], U8, "gs%d" % h, tag=("tabw1", "w1head01")[h])
+            nc.vector.tensor_copy(gs[h][:], tabs[:].indirect(idx[:, 32 * h : 32 * (h + 1)]))
+
+        dealt = {(0, u): tile([P, 2, 1024], BF16, "dealt0%d" % u, tag=("square0", "woven1")[u])[:] for u in range(2)}
         w1c = [tile([P, 1024], U32, "w1c0")]
-        w1s = [tile([P, 1024], U8, "w1s%d" % g) for g in range(2)]
+        w1s = [tile([P, 1024], U8, "w1s0")]
 
-        def deal(g, u, a, engine_copy=nc.scalar.copy):
-            dst = dealt[g][:, u, a, :].rearrange("p (t m j) -> p m j t", t=2, j=4)
-            src = w1raw[g][a][:].rearrange("p j (m t) -> p m j t", t=4)[:, :, :, 2 * u : 2 * u + 2]
-            engine_copy(dst, src)
+        def deal(g, u, a):
+            if g == 0:
+                dst = dealt[g, u][:, a, :].rearrange("p (c i j) -> p c j i", i=4, j=4)
+                src = w1head[u, a][:].rearrange("p j (c i) -> p c j i", i=4)
+            else:
+                dst = dealt[g, u][:, a, :].rearrange("p (t m j) -> p m j t", t=2, j=4)
+                src = w1raw[a][:].rearrange("p j (m t) -> p m j t", t=4)[:, :, :, 2 * u : 2 * u + 2]
+            nc.scalar.copy(dst, src)
 
         def quant_w1(g, first, count):
             cols = slice(256 * first, 256 * (first + count))
             nc.vector.quantize_mx(
                 out=w1c[g][:, cols].bitcast(FP8X4),
                 scales=w1s[g][:, cols],
-                in_=dealt[g][:].rearrange("p u a c -> p (u a c)")[:, 1024 * first : 1024 * (first + count)],
+                in_=dealt[g, first // 2].rearrange("p a c -> p (a c)")[:, 1024 * (first % 2) : 1024 * (first % 2 + count)],
             )
 
         deal(0, 0, 0)
         quant_w1(0, 0, 1)
-        deal(0, 0, 1, nc.vector.tensor_copy)
+        gather_scales(0)
+        deal(0, 0, 1)
         quant_w1(0, 1, 1)
-        deal(0, 1, 0)
-        deal(0, 1, 1)
-        turn_wg(1, spreads[1])
+        gather_scales(1)
+        for a in range(2):
+            deal(0, 1, a)
+        quant_w1(0, 2, 2)
 
-        def left_tile(i):
+        def left_half(i, h):
             g, u, e = i // 4, (i % 4) // 2, i % 2
-            banks = [psum.tile([P, BANK], F32, name="left", tag="bank%d" % (2 * (i % 2) + h)) for h in range(2)]
+            acc = psum.tile([P, BANK], F32, name="left", tag="bank%d" % (2 * (i % 2) + h))
             for a in range(2):
-                for h in range(2):
-                    acc = banks[h]
-                    cols = slice(512 * u + 256 * a + P * e, 512 * u + 256 * a + P * (e + 1))
-                    nc.tensor.matmul_mx(
-                        out=acc[:],
-                        lhsT=w1c[g][:, cols].bitcast(FP8X4),
-                        lhsT_scale=w1s[g][:, cols],
-                        rhs=gw[a][:, halves[h]].bitcast(FP8X4),
-                        rhs_scale=gs[4 * a : P, halves[h]],
-                        start=(a == 0),
-                        stop=(a == 1),
-                    )
-            return banks
+                cols = slice(512 * u + 256 * a + P * e, 512 * u + 256 * a + P * (e + 1))
+                nc.tensor.matmul_mx(
+                    out=acc[:],
+                    lhsT=w1c[g][:, cols].bitcast(FP8X4),
+                    lhsT_scale=w1s[g][:, cols],
+                    rhs=gw[a][:, halves[h]].bitcast(FP8X4),
+                    rhs_scale=gs[h][4 * a : P, :],
+                    start=(a == 0),
+                    stop=(a == 1),
+                )
+            return acc
+
+        def left_tiles(i):
+            square = tile([P, S], F32, "square", tag=SQUARE_TAGS.get(i, "square%d" % (i % 3)))
+            plain = ring.tile([P, S], F32, name="plain", tag="plain", align_bytes=64)
+            return square, plain
+
+        def copy_half(i, h, bank):
+            square, plain = left[i][0], left[i][1]
+            nc.scalar.activation(square[:, halves[h]], bank[:], ACT.Square)
+            nc.scalar.copy(plain[:, halves[h]], bank[:])
 
         def copy_left(i):
-            banks = left_tile(i)
-            mixed = ring.tile([P, S], F32, name="mixed", tag="mixed", align_bytes=64)
-            plain = ring.tile([P, BANK], F32, name="plain", tag="plain", align_bytes=64)
-            nc.scalar.copy(mixed[:, halves[0]], banks[0][:])
-            nc.scalar.activation(mixed[:, halves[1]], banks[1][:], ACT.Square)
-            nc.scalar.copy(plain[:], banks[1][:])
-            return mixed, plain
+            banks = [left_half(i, h) for h in range(2)]
+            left[i] = left_tiles(i) + (banks[0],)
+            for h in range(1 if i in SHARED else 0, 2):
+                copy_half(i, h, banks[h])
 
-        def wg_rows(i):
-            return wg[i % 4][:]
+        def factor(i):
+            return wg_plain[:] if i < 4 else wg[i - 4][:]
 
         def scatter(i):
-            nc.vector.tensor_copy(page[i][:].indirect(idx2[:]), (first_values[0] if i == 0 else rt[i])[:])
-            nc.sync.dma_start(rows_out1[i // 4, i % 4], page[i][:])
+            nc.vector.tensor_copy(page[i][:].indirect(idx2[:]), rt[i][:])
+            nc.sync.dma_start(rows(out_1, i), page[i][:])
 
-        def replace_first():
-            banks = left_tile(0)
-            u = tile([P, S], F32, "u")
-            for h in range(2):
-                nc.vector.tensor_tensor(u[:, halves[h]], banks[h][:], rt[0][:, halves[h]], ALU.mult)
-            for h in range(2):
-                nc.vector.scalar_tensor_tensor(u[:, halves[h]], u[:, halves[h]], -1.0, banks[h][:], ALU.add, ALU.mult)
-            return u
+        def first_products(h, bank):
+            nc.vector.tensor_tensor(u_first[:, halves[h]], bank[:], rt[0][:, halves[h]], ALU.mult)
+            nc.vector.scalar_tensor_tensor(
+                u_first[:, halves[h]], u_first[:, halves[h]], -1.0, bank[:], ALU.add, ALU.mult
+            )
 
-        def replace(i, mixed, plain):
-            lo, hi = halves
-            u = tile([P, S], F32, "u")
-            nc.gpsimd.tensor_tensor(u[:], mixed[:], rt[i][:], ALU.mult)
-            nc.gpsimd.tensor_tensor(mixed[:, hi], u[:, hi], plain[:], ALU.subtract)
-            nc.gpsimd.tensor_tensor(rt[i][:], mixed[:], wg_rows(i), ALU.mult)
-            nc.vector.scalar_tensor_tensor(rt[i][:, lo], u[:, lo], -1.0, rt[i][:, lo], ALU.add, ALU.mult)
+        def share(i):
+            square, bank = left[i][0], left[i][2]
+            shared = tile([P, BANK], F32, "shared%d" % i, tag=SHARED[i])
+            nc.vector.tensor_tensor(shared[:], bank[:], rt[i][:, halves[0]], ALU.mult)
+            nc.vector.scalar_tensor_tensor(square[:, halves[0]], shared[:], -1.0, bank[:], ALU.add, ALU.mult)
 
-        plane_tags = [["w1raw11", "woven1"], ["w1raw00", "w1raw01"]]
-        planes = {}
+        def replace(i):
+            square, plain = left[i][0], left[i][1]
+            own = halves[1] if i in SHARED else slice(0, S)
+            u = tile([P, S], F32, "work", tag=WORK_TAGS[i])
+            nc.gpsimd.tensor_tensor(u[:, own], square[:, own], rt[i][:, own], ALU.mult)
+            if i in SHARED:
+                nc.gpsimd.tensor_tensor(square[:, own], u[:, own], plain[:, own], ALU.subtract)
+                nc.gpsimd.tensor_tensor(rt[i][:], square[:], factor(i), ALU.mult)
+            else:
+                nc.gpsimd.tensor_tensor(u[:], u[:], plain[:], ALU.subtract)
+                nc.gpsimd.tensor_tensor(rt[i][:], u[:], factor(i), ALU.mult)
+
+        planes, crossed = {}, {}
 
         def round_plane(i, cols, engine_copy):
-            g, c = i // 4, cols.start // 1024
-            if (g, c) not in planes:
-                planes[g, c] = tile([P, 4, 1024], BF16, "planes%d%d" % (g, c), tag=plane_tags[g][c])
-            engine_copy(planes[g, c][:, i % 4, cols.start - 1024 * c : cols.stop - 1024 * c], page[i][:, cols])
+            b = cols.start // BANK
+            if b not in planes:
+                planes[b] = tile([P, 4, BANK], BF16, "planes%d" % b, tag="w1head%d%d" % (b // 2, b % 2))
+            engine_copy(planes[b][:, i - 4, cols.start - BANK * b : cols.stop - BANK * b], page[i][:, cols])
 
-        def round_page(i):
-            for c in range(2):
-                round_plane(i, slice(1024 * c, 1024 * (c + 1)), nc.scalar.copy)
-
-        def weave(engine_copy, woven, g, cols):
-            c = cols.start // 1024
-            engine_copy(
+        def weave(woven, cols):
+            b = cols.start // BANK
+            nc.vector.tensor_copy(
                 woven.rearrange("p (c i t) -> p c t i", i=4, t=4),
-                planes[g, c][:, :, cols.start - 1024 * c : cols.stop - 1024 * c].rearrange("p t (c i) -> p c t i", i=4),
+                planes[b][:, :, cols.start - BANK * b : cols.stop - BANK * b].rearrange("p t (c i) -> p c t i", i=4),
             )
+
+        def cross(i):
+            for b in range(4):
+                if b // 2 not in crossed:
+                    crossed[b // 2] = tile([P, 8, 4, P], BF16, "crossed%d" % (b // 2), tag=("w1raw11", "u")[b // 2])
+                bank = psum.tile([P, 4, P], F32, name="cross", tag="bank%d" % (4 + b))
+                for c in range(4):
+                    first_col = BANK * b + P * c
+                    nc.tensor.transpose(bank[:, c, :], page[i][:, first_col : first_col + P], ident[:])
+                nc.scalar.copy(crossed[b // 2][:, 4 * (b % 2) : 4 * (b % 2 + 1), i, :], bank[:])
+
+        def cross_back(woven, half):
+            for b in range(4):
+                bank = psum.tile([P, 2, 4, P], BF16, name="cross_back", tag="bank%d" % (4 + b))
+                for c in range(2):
+                    block = crossed[half][:, 2 * b + c].rearrange("p i (q t) -> p t (i q)", t=4)
+                    for t in range(4):
+                        nc.tensor.transpose(bank[:, c, t, :], block[:, t, :], ident_bf[:])
+                nc.scalar.copy(
+                    woven[:, 1024 * b : 1024 * (b + 1)].rearrange("p (c m t) -> p c m t", c=2, t=4),
+                    bank[:].rearrange("p c t m -> p c m t"),
+                )
 
         codes = {}
         scales = [tile([P, T2], U8, "scales%d" % g) for g in range(2)]
@@ -237,57 +277,85 @@ def tile_list_turf_probe_page_kernel(
                     out_3[g, 4 * q : 4 * q + 4, :].bitcast(I32), scales[g][32 * q : 32 * q + 4, :].bitcast(I32)
                 )
 
-        u_first = replace_first()
-        left = {1: copy_left(1)}
-        quant_w1(0, 2, 2)
-        first_values = [tile([P, S], F32, "first_values", tag="woven1")]
-        for h in range(2):
-            nc.vector.tensor_tensor(first_values[0][:, halves[h]], u_first[:, halves[h]], wg[0][:, halves[h]], ALU.mult)
+        u_first = tile([P, S], F32, "u")
+        first_products(0, left_half(0, 0))
+        left = {1: left_tiles(1) + (left_half(1, 0),)}
+        share(1)
+        first_products(1, left_half(0, 1))
+        copy_half(1, 1, left_half(1, 1))
+        for h, engine in enumerate((nc.gpsimd, nc.vector)):
+            engine.tensor_tensor(rt[0][:, halves[h]], u_first[:, halves[h]], wg_plain[:, halves[h]], ALU.mult)
+        replace(1)
         scatter(0)
-        left[2] = copy_left(2)
-        turn_wg(2, spread_wg(2))
-        left[3] = copy_left(3)
-        turn_wg(3, spread_wg(3))
-        dealt.append(tile([P, 2, 2, 1024], BF16, "dealt1", tag="woven1"))
+        copy_left(2)
+        for u in range(2):
+            dealt[1, u] = tile([P, 2, 1024], BF16, "dealt1%d" % u, tag=("u", "w1head00")[u])[:]
         for a in range(2):
             for u in range(2):
                 deal(1, u, a)
+        copy_left(3)
+        for c in range(8):
+            nc.tensor.transpose(turned[c // 4][:, c % 4, :], wg_plain[:, P * c : P * (c + 1)], ident[:])
+        for t in range(4):
+            turn_wg(t, spread_wg(t))
+        for i in range(6, 8):
+            rt.append(tile([P, S], F32, "right%d" % i))
+            load_right(i)
+            load_page(i)
+        for q in range(4):
+            nc.sync.dma_start(
+                w2s[32 * q : 32 * q + 4, :, :].bitcast(I32),
+                w2_scales[:, 4 * q : 4 * q + 4, :].rearrange("a r c -> r a c").bitcast(I32),
+            )
         for i in range(1, 8):
-            replace(i, *left[i])
             if i == 7:
                 codes[0] = tile([P, T2], U32, "codes0", tag="right6")
                 for c in range(2):
                     quantize_page(0, slice(1024 * c, 1024 * (c + 1)), first[c][:], codes[0][:, 1024 * c : 1024 * (c + 1)])
                 store_scales(0)
+            if i == 3:
+                w2w = tile([P, 2, 2 * N], U8, "w2w", tag="wg_plain")
+                nc.sync.dma_start(w2w[:].bitcast(I32), w2_words.rearrange("a p c -> p a c").bitcast(I32))
+                share(4)
             scatter(i)
             if i == 1:
+                replace(2)
                 w1c.append(tile([P, 1024], U32, "w1c1", tag="right1"))
-                quant_w1(1, 0, 4)
+                w1s.append(tile([P, 1024], U8, "w1s1", tag="w1head11"))
+                quant_w1(1, 0, 2)
+                quant_w1(1, 2, 2)
+            elif i < 7:
+                replace(i + 1)
             if i + 3 < 8:
-                left[i + 3] = copy_left(i + 3)
-            round_page(i - 1)
+                copy_left(i + 3)
+            if i <= 4:
+                cross(i - 1)
+            for b in range(4 if i > 4 else 0):
+                round_plane(i - 1, slice(BANK * b, BANK * (b + 1)), nc.scalar.copy)
             if i == 4:
                 first = [tile([P, 4096], BF16, "woven0%d" % c, tag="tabw%d" % c) for c in range(2)]
-                for b in range(4):
-                    weave(nc.scalar.copy, first[b // 2][:, 2048 * (b % 2) : 2048 * (b % 2 + 1)], 0, slice(BANK * b, BANK * (b + 1)))
+                for c in range(2):
+                    cross_back(first[c][:], c)
 
         edges = [sum(CHUNKS[:c]) for c in range(len(CHUNKS) + 1)]
         chunks = [slice(edges[c], edges[c + 1]) for c in range(len(CHUNKS))]
+        units = [(c, n0, BANK // w) for c, w in enumerate(CHUNKS) for n0 in range(0, 4, BANK // w)]
         accs = {}
 
         def product(k, g):
-            c, n = k // 4, k % 4
+            c, n0, count = units[k]
             if g == 0:
-                accs[k] = psum.tile([P, BANK], F32, name="prod", tag="bank%d" % (k % 8))[:, 0 : CHUNKS[c]]
-            nc.tensor.matmul_mx(
-                out=accs[k],
-                lhsT=w2w[:, g, 2 * P * n : 2 * P * (n + 1)].bitcast(FP4X4),
-                lhsT_scale=w2s[:, g, P * n : P * (n + 1)],
-                rhs=(codes[0][:, chunks[c]] if g == 0 else last_codes[c][:]).bitcast(FP8X4),
-                rhs_scale=scales[g][:, chunks[c]],
-                start=(g == 0),
-                stop=(g == 1),
-            )
+                accs[k] = psum.tile([P, count, CHUNKS[c]], F32, name="prod", tag="bank%d" % (k % 8))
+            for n in range(n0, n0 + count):
+                nc.tensor.matmul_mx(
+                    out=accs[k][:, n - n0, :],
+                    lhsT=w2w[:, g, 2 * P * n : 2 * P * (n + 1)].bitcast(FP4X4),
+                    lhsT_scale=w2s[:, g, P * n : P * (n + 1)],
+                    rhs=(codes[0][:, chunks[c]] if g == 0 else last_codes[c][:]).bitcast(FP8X4),
+                    rhs_scale=scales[g][:, chunks[c]],
+                    start=(g == 0 and n == n0),
+                    stop=(g == 1 and n == n0 + count - 1),
+                )
 
         for k in range(8):
             product(k, 0)
@@ -299,33 +367,53 @@ def tile_list_turf_probe_page_kernel(
         for c in range(len(CHUNKS)):
             round_plane(7, chunks[c], nc.vector.tensor_copy if c < 2 else nc.scalar.copy)
         for c, cols in enumerate(chunks):
-            weave(nc.vector.tensor_copy, last[c][:], 1, cols)
+            weave(last[c][:], cols)
             quantize_page(1, cols, last[c][:], last_codes[c][:])
         store_scales(1)
 
         rows_out0 = out_0.rearrange("(n p) m -> p n m", p=P)
-        early = tile([P, 2, 4, 256], F32, "staged_early", tag="w1raw10")
+        early = tile([P, 4, BANK], F32, "staged_early", tag="w1raw10")
         middle = tile([P, 4, BANK], F32, "staged_middle", tag="w1raw11")
-        late = tile([P, 2, 4, BANK], F32, "staged_late", tag="woven1")
-        staged = [early[:, 0], early[:, 1], middle[:], late[:, 0], late[:, 1]]
-        roles = "SSSSSSSSSSSSGGGGGVVV"
-        for k in range(4 * len(CHUNKS)):
-            c, n = k // 4, k % 4
-            if k >= 8:
-                product(k, 0)
+        late = tile([P, 8, BANK], F32, "staged_late", tag="woven1")
+
+        def staged(k, first_row, stop_row):
+            home, base = (early, 0) if k < 4 else (middle, 4) if k < 8 else (late, 8)
+            row0 = 4 * (k // 4) - base
+            return home[:, row0 + first_row : row0 + stop_row, :]
+
+        for k in range(8):
             product(k, 1)
-            y = staged[c][:, n, :]
-            acc = accs[k]
-            if roles[k] == "S":
+        def values(k):
+            c, n0, count = units[k]
+            first_col = edges[c] % BANK
+            return staged(k, n0, n0 + count)[:, :, first_col : first_col + CHUNKS[c]]
+
+        def square_bank(k):
+            y, acc = values(k), accs[k][:]
+            if ROLES[k] == "S":
                 nc.scalar.activation(y, acc, ACT.Square)
-            elif roles[k] == "G":
+            elif ROLES[k] == "G":
                 nc.vector.tensor_copy(y, acc)
                 nc.gpsimd.tensor_tensor(y, y, y, ALU.mult)
             else:
                 nc.vector.tensor_copy(y, acc)
                 nc.vector.tensor_tensor(y, acc, y, ALU.mult)
-            nc.scalar.activation(y, y, ACT.Ln, bias=1.0)
-            per_store = 4 if c < 2 else (2 if c < 4 else 1)
-            if (n + 1) % per_store == 0:
-                rows = slice(n + 1 - per_store, n + 1)
-                nc.sync.dma_start(rows_out0[:, rows, chunks[c]], staged[c][:, rows, :])
+
+        def finish_bank(k):
+            nc.scalar.activation(values(k), values(k), ACT.Ln, bias=1.0)
+            if k in STORES:
+                first_row, stop_row = STORES[k]
+                block = k // 4
+                nc.sync.dma_start(
+                    rows_out0[:, first_row:stop_row, BANK * block : BANK * (block + 1)], staged(k, first_row, stop_row)
+                )
+
+        for k in range(8):
+            square_bank(k)
+            finish_bank(k)
+        for k in SQUARE_ORDER:
+            product(k, 0)
+            product(k, 1)
+            square_bank(k)
+        for k in FINISH_ORDER:
+            finish_bank(k)

@@ -22,10 +22,13 @@ BANK = 512
 SHARED = {1: "square0", 4: "right2"}
 WORK_TAGS = {1: "u", 2: "w1head11", 3: "w1head00", 4: "w1head00", 5: "w1c0", 6: "w1c0", 7: "w1c0"}
 SQUARE_TAGS = {1: "w1head11", 4: "w1c0", 7: "woven1"}
-CHUNKS = (256, 256, 512, 512, 512)
-ROLES = "SSSSSSSSGGGVGVVV"
-SQUARE_ORDER = range(8, 16)
-FINISH_ORDER = (8, 9, 11, 10, 13, 12, 14, 15)
+CHUNKS = (128, 128, 256, 512, 512, 512)
+WOVEN_TAGS = ("right2", "right3", "right4", "right5", "woven14", "square2")
+CODE_TAGS = ("w1s0", "gw0", "gw1", "w1c0", "right1", "square0")
+SCALAR_CHUNK = 3
+ROLES = "SSSSSSSGGGVGVGVV"
+ON_SCALAR = 7
+FINISH_ORDER = (7, 8, 10, 9, 12, 11, 14, 13, 15)
 STORES = {2: (0, 2), 3: (2, 4), 4: (0, 1), 5: (1, 2), 6: (2, 3), 7: (3, 4), 8: (0, 1), 9: (1, 2), 10: (2, 3), 11: (3, 4), 12: (0, 1), 13: (1, 2), 14: (2, 3), 15: (3, 4)}
 
 
@@ -54,7 +57,6 @@ def tile_list_turf_probe_page_kernel(
         w2s = tile([P, 2, N], U8, "w2s")
         warm = tile([P, 1], F32, "warm")
         ident = tile([P, P], F32, "ident")
-        ident_bf = tile([P, P], BF16, "ident_bf")
         wg_plain = tile([P, S], F32, "wg_plain")
 
         def rows(matrix, i):
@@ -87,7 +89,6 @@ def tile_list_turf_probe_page_kernel(
                 tabs[32 * q : 32 * q + 8, :].bitcast(I32), tab_scales[:, 4 * q : 4 * q + 4, :].bitcast(I32)
             )
         make_identity(nc, ident[:])
-        make_identity(nc, ident_bf[:])
         for a in range(2):
             load_w1(w1head[0, a], a, slice(0, 256))
         load_right(0)
@@ -215,6 +216,11 @@ def tile_list_turf_probe_page_kernel(
             nc.vector.tensor_tensor(shared[:], bank[:], rt[i][:, halves[0]], ALU.mult)
             nc.vector.scalar_tensor_tensor(square[:, halves[0]], shared[:], -1.0, bank[:], ALU.add, ALU.mult)
 
+        last_values = []
+
+        def scatter_last(h):
+            nc.vector.tensor_copy(page[7][:].indirect(idx2[:, 32 * h : 32 * (h + 1)]), last_values[h])
+
         def replace(i):
             square, plain = left[i][0], left[i][1]
             own = halves[1] if i in SHARED else slice(0, S)
@@ -225,43 +231,64 @@ def tile_list_turf_probe_page_kernel(
                 nc.gpsimd.tensor_tensor(rt[i][:], square[:], factor(i), ALU.mult)
             else:
                 nc.gpsimd.tensor_tensor(u[:], u[:], plain[:], ALU.subtract)
-                nc.gpsimd.tensor_tensor(rt[i][:], u[:], factor(i), ALU.mult)
+                if i < 7:
+                    nc.gpsimd.tensor_tensor(rt[i][:], u[:], factor(i), ALU.mult)
+                else:
+                    last_values.append(tile([P, BANK], F32, "last_low", tag="right0")[:])
+                    last_values.append(rt[i][:, halves[1]])
+                    for h in range(2):
+                        nc.gpsimd.tensor_tensor(last_values[h], u[:, halves[h]], wg[3][:, halves[h]], ALU.mult)
 
         planes, crossed = {}, {}
 
         def round_plane(i, cols, engine_copy):
             b = cols.start // BANK
             if b not in planes:
-                planes[b] = tile([P, 4, BANK], BF16, "planes%d" % b, tag="w1head%d%d" % (b // 2, b % 2))
+                planes[b] = tile([P, 2, BANK], BF16, "planes%d" % b, tag="w1head%d%d" % (b // 2, b % 2))
             engine_copy(planes[b][:, i - 4, cols.start - BANK * b : cols.stop - BANK * b], page[i][:, cols])
 
-        def weave(woven, cols):
-            b = cols.start // BANK
-            nc.vector.tensor_copy(
-                woven.rearrange("p (c i t) -> p c t i", i=4, t=4),
-                planes[b][:, :, cols.start - BANK * b : cols.stop - BANK * b].rearrange("p t (c i) -> p c t i", i=4),
-            )
+        edges = [sum(CHUNKS[:c]) for c in range(len(CHUNKS) + 1)]
+        chunks = [slice(edges[c], edges[c + 1]) for c in range(len(CHUNKS))]
+        last = []
+
+        def place_low_pair(c):
+            cols, b = chunks[c], edges[c] // BANK
+            last.append(tile([P, CHUNKS[c], 4], BF16, "woven1%d" % c, tag=WOVEN_TAGS[c]))
+            pair = planes[b][:, :, cols.start - BANK * b : cols.stop - BANK * b]
+            nc.scalar.copy(last[c][:, :, 0:2], pair.rearrange("p t m -> p m t"))
+
+        def place_third(c):
+            nc.scalar.copy(last[c][:, :, 2:4], page[6][:, chunks[c]].unsqueeze(2).to_broadcast([P, CHUNKS[c], 2]))
+
+        def place_fourth(c):
+            engine_copy = nc.scalar.copy if c == SCALAR_CHUNK else nc.vector.tensor_copy
+            engine_copy(last[c][:, :, 3], page[7][:, chunks[c]])
 
         def cross(i):
             for b in range(4):
                 if b // 2 not in crossed:
-                    crossed[b // 2] = tile([P, 8, 4, P], BF16, "crossed%d" % (b // 2), tag=("w1raw11", "u")[b // 2])
-                bank = psum.tile([P, 4, P], F32, name="cross", tag="bank%d" % (4 + b))
+                    crossed[b // 2] = tile([P, 8, 2, 4, 32, 2], BF16, "crossed%d" % (b // 2), tag=("w1raw11", "u")[b // 2])
+                turned_rows = psum.tile([P, 4, P], F32, name="cross", tag="bank%d" % (4 + b))
                 for c in range(4):
                     first_col = BANK * b + P * c
-                    nc.tensor.transpose(bank[:, c, :], page[i][:, first_col : first_col + P], ident[:])
-                nc.scalar.copy(crossed[b // 2][:, 4 * (b % 2) : 4 * (b % 2 + 1), i, :], bank[:])
+                    nc.tensor.transpose(turned_rows[:, c, :], page[i][:, first_col : first_col + P], ident[:])
+                nc.scalar.copy(
+                    crossed[b // 2][:, 4 * (b % 2) : 4 * (b % 2 + 1), :, i, :, :],
+                    turned_rows[:].rearrange("p c (q u e) -> p c u q e", u=2, e=2),
+                )
 
         def cross_back(woven, half):
+            words = crossed[half][:].rearrange("p c u i q e -> p (c u i q e)").bitcast(F32)
+            woven_words = woven.bitcast(F32)
             for b in range(4):
-                bank = psum.tile([P, 2, 4, P], BF16, name="cross_back", tag="bank%d" % (4 + b))
+                pairs = psum.tile([P, 2, 2, P], F32, name="cross_back", tag="bank%d" % (4 + b))
                 for c in range(2):
-                    block = crossed[half][:, 2 * b + c].rearrange("p i (q t) -> p t (i q)", t=4)
-                    for t in range(4):
-                        nc.tensor.transpose(bank[:, c, t, :], block[:, t, :], ident_bf[:])
+                    for u in range(2):
+                        first_word = P * (2 * (2 * b + c) + u)
+                        nc.tensor.transpose(pairs[:, c, u, :], words[:, first_word : first_word + P], ident[:])
                 nc.scalar.copy(
-                    woven[:, 1024 * b : 1024 * (b + 1)].rearrange("p (c m t) -> p c m t", c=2, t=4),
-                    bank[:].rearrange("p c t m -> p c m t"),
+                    woven_words[:, 512 * b : 512 * (b + 1)].rearrange("p (c m u) -> p c m u", c=2, u=2),
+                    pairs[:].rearrange("p c u m -> p c m u"),
                 )
 
         codes = {}
@@ -309,7 +336,8 @@ def tile_list_turf_probe_page_kernel(
             )
         for i in range(1, 8):
             if i == 7:
-                codes[0] = tile([P, T2], U32, "codes0", tag="right6")
+                scatter_last(0)
+                codes[0] = tile([P, T2], U32, "codes0", tag="right0")
                 for c in range(2):
                     quantize_page(0, slice(1024 * c, 1024 * (c + 1)), first[c][:], codes[0][:, 1024 * c : 1024 * (c + 1)])
                 store_scales(0)
@@ -317,7 +345,11 @@ def tile_list_turf_probe_page_kernel(
                 w2w = tile([P, 2, 2 * N], U8, "w2w", tag="wg_plain")
                 nc.sync.dma_start(w2w[:].bitcast(I32), w2_words.rearrange("a p c -> p a c").bitcast(I32))
                 share(4)
-            scatter(i)
+            if i < 7:
+                scatter(i)
+            else:
+                scatter_last(1)
+                nc.sync.dma_start(rows(out_1, 7), page[7][:])
             if i == 1:
                 replace(2)
                 w1c.append(tile([P, 1024], U32, "w1c1", tag="right1"))
@@ -330,15 +362,17 @@ def tile_list_turf_probe_page_kernel(
                 copy_left(i + 3)
             if i <= 4:
                 cross(i - 1)
-            for b in range(4 if i > 4 else 0):
+            for b in range(4 if i in (5, 6) else 0):
                 round_plane(i - 1, slice(BANK * b, BANK * (b + 1)), nc.scalar.copy)
+            for c in range(len(CHUNKS) if i == 6 else 0):
+                place_low_pair(c)
+            for c in range(len(CHUNKS) if i == 7 else 0):
+                place_third(c)
             if i == 4:
                 first = [tile([P, 4096], BF16, "woven0%d" % c, tag="tabw%d" % c) for c in range(2)]
                 for c in range(2):
                     cross_back(first[c][:], c)
 
-        edges = [sum(CHUNKS[:c]) for c in range(len(CHUNKS) + 1)]
-        chunks = [slice(edges[c], edges[c + 1]) for c in range(len(CHUNKS))]
         units = [(c, n0, BANK // w) for c, w in enumerate(CHUNKS) for n0 in range(0, 4, BANK // w)]
         accs = {}
 
@@ -360,15 +394,14 @@ def tile_list_turf_probe_page_kernel(
         for k in range(8):
             product(k, 0)
 
-        woven_tags = ["right2", "right3", "right4", "right5", "woven1"]
-        code_tags = ["gw0", "gw1", "w1c0", "right0", "right1"]
-        last = [tile([P, 4 * w], BF16, "woven1%d" % c, tag=woven_tags[c]) for c, w in enumerate(CHUNKS)]
-        last_codes = [tile([P, w], U32, "codes1%d" % c, tag=code_tags[c]) for c, w in enumerate(CHUNKS)]
-        for c in range(len(CHUNKS)):
-            round_plane(7, chunks[c], nc.vector.tensor_copy if c < 2 else nc.scalar.copy)
+        last_codes = [tile([P, w], U32, "codes1%d" % c, tag=CODE_TAGS[c]) for c, w in enumerate(CHUNKS)]
+        place_fourth(SCALAR_CHUNK)
+        ahead = [c for c in range(len(CHUNKS)) if c != SCALAR_CHUNK]
+        place_fourth(ahead[0])
         for c, cols in enumerate(chunks):
-            weave(last[c][:], cols)
-            quantize_page(1, cols, last[c][:], last_codes[c][:])
+            if c + 1 < len(ahead):
+                place_fourth(ahead[c + 1])
+            quantize_page(1, cols, last[c][:].rearrange("p m t -> p (m t)"), last_codes[c][:])
         store_scales(1)
 
         rows_out0 = out_0.rearrange("(n p) m -> p n m", p=P)
@@ -408,12 +441,13 @@ def tile_list_turf_probe_page_kernel(
                     rows_out0[:, first_row:stop_row, BANK * block : BANK * (block + 1)], staged(k, first_row, stop_row)
                 )
 
-        for k in range(8):
+        for k in range(ON_SCALAR):
             square_bank(k)
             finish_bank(k)
-        for k in SQUARE_ORDER:
-            product(k, 0)
-            product(k, 1)
+        for k in range(ON_SCALAR, 16):
+            if k >= 8:
+                product(k, 0)
+                product(k, 1)
             square_bank(k)
         for k in FINISH_ORDER:
             finish_bank(k)

@@ -20,12 +20,16 @@ ACT = mybir.ActivationFunctionType
 P = 128
 BANK = 512
 SHARED = {1: "square0", 4: "right2"}
-WORK_TAGS = {1: "u", 2: "w1head11", 3: "w1head00", 4: "w1head00", 5: "w1c0", 6: "w1c0", 7: "w1c0"}
-SQUARE_TAGS = {1: "w1head11", 4: "w1c0", 7: "woven1"}
+PLACES = {4: (1, 0), 5: (0, 0), 6: (0, 1), 7: (1, 1)}
+FACTORS = {4: 0, 5: 1, 6: 1, 7: 2}
+WORK_TAGS = {1: "u", 2: "right1", 3: "w1head00", 4: "w1head00", 5: "w1c0", 6: "w1c0", 7: "w1c0"}
+SQUARE_TAGS = {1: "woven14", 4: "w1c0", 7: "w1head00"}
 CHUNKS = (128, 128, 256, 512, 512, 512)
 WOVEN_TAGS = ("right2", "right3", "right4", "right5", "woven14", "square2")
 CODE_TAGS = ("w1s0", "gw0", "gw1", "w1c0", "right1", "square0")
-SCALAR_CHUNK = 3
+BACK_BANKS = (4, 5, 6, 7, 4, 3, 2, 1, 0)
+AHEAD = 4
+SCALAR_CHUNK = 5
 ROLES = "SSSSSSSGGGVGVGVV"
 ON_SCALAR = 7
 FINISH_ORDER = (7, 8, 10, 9, 12, 11, 14, 13, 15)
@@ -51,8 +55,8 @@ def tile_list_turf_probe_page_kernel(
         tabs = tile([P, T], U8, "tabs")
         w1head = {(u, a): tile([P, 4, 256], F32, "w1head%d%d" % (u, a)) for u in range(2) for a in range(2)}
         w1raw = [tile([P, 4, 512], F32, "w1raw1%d" % a) for a in range(2)]
-        rt = [tile([P, S], F32, "right%d" % i) for i in range(6)]
-        wg = [tile([P, S], F32, "wg%d" % t) for t in range(4)]
+        rt = [tile([P, S], F32, "right%d" % i) for i in range(8)]
+        wg = [tile([P, S], F32, "wg%d" % t) for t in range(3)]
         page = [tile([P, T2], F32, "page%d" % i) for i in range(8)]
         w2s = tile([P, 2, N], U8, "w2s")
         warm = tile([P, 1], F32, "warm")
@@ -62,7 +66,9 @@ def tile_list_turf_probe_page_kernel(
         def rows(matrix, i):
             if i < 4:
                 return matrix[P * i : P * (i + 1), :]
-            return matrix[512:1024, :].rearrange("(p t) m -> t p m", t=4)[i - 4]
+            if i in (5, 6):
+                return matrix[256 * (i - 3) : 256 * (i - 2), :].rearrange("(p t) m -> p t m", t=4)[:, 0:2, :]
+            return matrix[512:1024, :].rearrange("(p t) m -> t p m", t=4)[2 if i == 4 else 3]
 
         nc.vector.memset(tabs[:].bitcast(I32), 0)
         nc.vector.memset(warm[:], 1.0)
@@ -91,38 +97,46 @@ def tile_list_turf_probe_page_kernel(
         make_identity(nc, ident[:])
         for a in range(2):
             load_w1(w1head[0, a], a, slice(0, 256))
+        halves = [slice(0, BANK), slice(BANK, S)]
         load_right(0)
-        nc.sync.dma_start(rt[1][:, 0:BANK], rows(right, 1)[:, 0:BANK])
-        for a in range(2):
-            load_w1(w1head[1, a], a, slice(256, 512))
-        nc.sync.dma_start(wg_plain[:], wgs)
+        nc.sync.dma_start(wg_plain[:, halves[0]], wgs[:, halves[0]])
+        load_right(1)
         nc.sync.dma_start(idx2[:], offs2)
         load_page(0)
-        nc.sync.dma_start(rt[1][:, BANK:S], rows(right, 1)[:, BANK:S])
+        for a in range(2):
+            load_w1(w1head[1, a], a, slice(256, 512))
+        nc.sync.dma_start(wg_plain[:, halves[1]], wgs[:, halves[1]])
         load_right(2)
         load_page(1)
         for a in range(2):
             load_w1(w1raw[a], a, slice(512, 1024))
-        for i in range(3, 6):
+        for i in range(3, 8):
             load_right(i)
             load_page(i - 1)
-        load_page(5)
+        load_page(7)
 
-        halves = [slice(0, BANK), slice(BANK, S)]
         turned = [psum.tile([P, 4, P], F32, name="turned", tag="bank%d" % (6 + h)) for h in range(2)]
 
         def spread_wg(t):
-            spread = tile([P, 8, 4, 32], F32, "spread", tag="right%d" % (6 + t % 2))
+            spread = tile([P, 8, P], F32, "spread", tag="w1head10")
             for h in range(2):
-                rows = turned[h][:].rearrange("p c (q t) -> p c t q", t=4)[:, :, t : t + 1, :]
-                nc.scalar.copy(spread[:, 4 * h : 4 * (h + 1)], rows.to_broadcast([P, 4, 4, 32]))
+                part = spread[:, 4 * h : 4 * (h + 1), :]
+                if t == 1:
+                    picked = turned[h][:].rearrange("p c (q t) -> p c q t", t=4)[:, :, :, 0:2]
+                    nc.scalar.copy(
+                        part.rearrange("p c (a q e) -> p c a q e", a=2, e=2),
+                        picked.unsqueeze(2).to_broadcast([P, 4, 2, 32, 2]),
+                    )
+                else:
+                    picked = turned[h][:].rearrange("p c (q t) -> p c t q", t=4)[:, :, 2 + t // 2 : 3 + t // 2, :]
+                    nc.scalar.copy(part.rearrange("p c (a q) -> p c a q", a=4), picked.to_broadcast([P, 4, 4, 32]))
             return spread
 
         def turn_wg(t, spread):
             for h in range(2):
                 back = psum.tile([P, 4, P], F32, name="back", tag="bank%d" % (4 + h))
                 for c in range(4):
-                    nc.tensor.transpose(back[:, c, :], spread[:, 4 * h + c].rearrange("p a q -> p (a q)"), ident[:])
+                    nc.tensor.transpose(back[:, c, :], spread[:, 4 * h + c, :], ident[:])
                 nc.scalar.copy(wg[t][:, halves[h]], back[:].rearrange("p c j -> p (c j)"))
 
         gw = [tile([P, S], U32, "gw%d" % a) for a in range(2)]
@@ -135,7 +149,7 @@ def tile_list_turf_probe_page_kernel(
             nc.vector.tensor_copy(gs[h][:], tabs[:].indirect(idx[:, 32 * h : 32 * (h + 1)]))
 
         dealt = {(0, u): tile([P, 2, 1024], BF16, "dealt0%d" % u, tag=("square0", "woven1")[u])[:] for u in range(2)}
-        w1c = [tile([P, 1024], U32, "w1c0")]
+        w1c = {(0, 0): tile([P, 512], U32, "w1c0")[:]}
         w1s = [tile([P, 1024], U8, "w1s0")]
 
         def deal(g, u, a):
@@ -143,14 +157,14 @@ def tile_list_turf_probe_page_kernel(
                 dst = dealt[g, u][:, a, :].rearrange("p (c i j) -> p c j i", i=4, j=4)
                 src = w1head[u, a][:].rearrange("p j (c i) -> p c j i", i=4)
             else:
-                dst = dealt[g, u][:, a, :].rearrange("p (t m j) -> p m j t", t=2, j=4)
+                dst = dealt[g, u][:, a, :].rearrange(("p (m t j) -> p m j t", "p (t m j) -> p m j t")[u], t=2, j=4)
                 src = w1raw[a][:].rearrange("p j (m t) -> p m j t", t=4)[:, :, :, 2 * u : 2 * u + 2]
             nc.scalar.copy(dst, src)
 
         def quant_w1(g, first, count):
             cols = slice(256 * first, 256 * (first + count))
             nc.vector.quantize_mx(
-                out=w1c[g][:, cols].bitcast(FP8X4),
+                out=w1c[g, first // 2][:, 256 * (first % 2) : 256 * (first % 2 + count)].bitcast(FP8X4),
                 scales=w1s[g][:, cols],
                 in_=dealt[g, first // 2].rearrange("p a c -> p (a c)")[:, 1024 * (first % 2) : 1024 * (first % 2 + count)],
             )
@@ -161,18 +175,16 @@ def tile_list_turf_probe_page_kernel(
         deal(0, 0, 1)
         quant_w1(0, 1, 1)
         gather_scales(1)
-        for a in range(2):
-            deal(0, 1, a)
-        quant_w1(0, 2, 2)
 
         def left_half(i, h):
-            g, u, e = i // 4, (i % 4) // 2, i % 2
+            g = i // 4
+            u, e = PLACES.get(i, (i // 2, i % 2))
             acc = psum.tile([P, BANK], F32, name="left", tag="bank%d" % (2 * (i % 2) + h))
             for a in range(2):
                 cols = slice(512 * u + 256 * a + P * e, 512 * u + 256 * a + P * (e + 1))
                 nc.tensor.matmul_mx(
                     out=acc[:],
-                    lhsT=w1c[g][:, cols].bitcast(FP8X4),
+                    lhsT=w1c[g, u][:, 256 * a + P * e : 256 * a + P * (e + 1)].bitcast(FP8X4),
                     lhsT_scale=w1s[g][:, cols],
                     rhs=gw[a][:, halves[h]].bitcast(FP8X4),
                     rhs_scale=gs[h][4 * a : P, :],
@@ -194,21 +206,27 @@ def tile_list_turf_probe_page_kernel(
         def copy_left(i):
             banks = [left_half(i, h) for h in range(2)]
             left[i] = left_tiles(i) + (banks[0],)
-            for h in range(1 if i in SHARED else 0, 2):
-                copy_half(i, h, banks[h])
+            own = range(1 if i in SHARED else 0, 2)
+            for h in own:
+                nc.scalar.activation(left[i][0][:, halves[h]], banks[h][:], ACT.Square)
+            for h in own:
+                nc.scalar.copy(left[i][1][:, halves[h]], banks[h][:])
 
         def factor(i):
-            return wg_plain[:] if i < 4 else wg[i - 4][:]
+            return wg_plain[:] if i < 4 else wg[FACTORS[i]][:]
+
+        placed = {}
 
         def scatter(i):
-            nc.vector.tensor_copy(page[i][:].indirect(idx2[:]), rt[i][:])
+            nc.vector.tensor_copy(page[i][:].indirect(idx2[:]), placed.get(i, rt[i])[:])
             nc.sync.dma_start(rows(out_1, i), page[i][:])
 
+        def scatter_half(i, h, part):
+            nc.vector.tensor_copy(page[i][:].indirect(idx2[:, 32 * h : 32 * (h + 1)]), part)
+
         def first_products(h, bank):
-            nc.vector.tensor_tensor(u_first[:, halves[h]], bank[:], rt[0][:, halves[h]], ALU.mult)
-            nc.vector.scalar_tensor_tensor(
-                u_first[:, halves[h]], u_first[:, halves[h]], -1.0, bank[:], ALU.add, ALU.mult
-            )
+            nc.vector.tensor_tensor(u_first[h][:], bank[:], rt[0][:, halves[h]], ALU.mult)
+            nc.vector.scalar_tensor_tensor(u_first[h][:], u_first[h][:], -1.0, bank[:], ALU.add, ALU.mult)
 
         def share(i):
             square, bank = left[i][0], left[i][2]
@@ -218,47 +236,68 @@ def tile_list_turf_probe_page_kernel(
 
         last_values = []
 
-        def scatter_last(h):
-            nc.vector.tensor_copy(page[7][:].indirect(idx2[:, 32 * h : 32 * (h + 1)]), last_values[h])
-
         def replace(i):
             square, plain = left[i][0], left[i][1]
             own = halves[1] if i in SHARED else slice(0, S)
             u = tile([P, S], F32, "work", tag=WORK_TAGS[i])
+            if i == 7:
+                last_values.append(tile([P, BANK], F32, "last_low", tag="right0")[:])
+                last_values.append(rt[i][:, halves[1]])
+                for h, cols in enumerate(halves):
+                    nc.gpsimd.tensor_tensor(u[:, cols], square[:, cols], rt[i][:, cols], ALU.mult)
+                    nc.gpsimd.tensor_tensor(u[:, cols], u[:, cols], plain[:, cols], ALU.subtract)
+                    nc.gpsimd.tensor_tensor(last_values[h], u[:, cols], factor(i)[:, cols], ALU.mult)
+                return
             nc.gpsimd.tensor_tensor(u[:, own], square[:, own], rt[i][:, own], ALU.mult)
             if i in SHARED:
                 nc.gpsimd.tensor_tensor(square[:, own], u[:, own], plain[:, own], ALU.subtract)
-                nc.gpsimd.tensor_tensor(rt[i][:], square[:], factor(i), ALU.mult)
+                if i > 1:
+                    nc.gpsimd.tensor_tensor(rt[i][:], square[:], factor(i), ALU.mult)
             else:
                 nc.gpsimd.tensor_tensor(u[:], u[:], plain[:], ALU.subtract)
-                if i < 7:
-                    nc.gpsimd.tensor_tensor(rt[i][:], u[:], factor(i), ALU.mult)
-                else:
-                    last_values.append(tile([P, BANK], F32, "last_low", tag="right0")[:])
-                    last_values.append(rt[i][:, halves[1]])
-                    for h in range(2):
-                        nc.gpsimd.tensor_tensor(last_values[h], u[:, halves[h]], wg[3][:, halves[h]], ALU.mult)
+                nc.gpsimd.tensor_tensor(rt[i][:], u[:], factor(i), ALU.mult)
 
-        planes, crossed = {}, {}
-
-        def round_plane(i, cols, engine_copy):
-            b = cols.start // BANK
-            if b not in planes:
-                planes[b] = tile([P, 2, BANK], BF16, "planes%d" % b, tag="w1head%d%d" % (b // 2, b % 2))
-            engine_copy(planes[b][:, i - 4, cols.start - BANK * b : cols.stop - BANK * b], page[i][:, cols])
+        crossed = {}
 
         edges = [sum(CHUNKS[:c]) for c in range(len(CHUNKS) + 1)]
         chunks = [slice(edges[c], edges[c + 1]) for c in range(len(CHUNKS))]
         last = []
 
-        def place_low_pair(c):
-            cols, b = chunks[c], edges[c] // BANK
-            last.append(tile([P, CHUNKS[c], 4], BF16, "woven1%d" % c, tag=WOVEN_TAGS[c]))
-            pair = planes[b][:, :, cols.start - BANK * b : cols.stop - BANK * b]
-            nc.scalar.copy(last[c][:, :, 0:2], pair.rearrange("p t m -> p m t"))
+        def cross_late(i):
+            if i == 4:
+                crossed[2] = tile([P, 16, 2, P, 2], BF16, "crossed2", tag="woven1")
+            for b in range(4):
+                turned_rows = psum.tile([P, 4, P], F32, name="cross", tag="bank%d" % (4 + b))
+                for c in range(4):
+                    first_col = BANK * b + P * c
+                    nc.tensor.transpose(turned_rows[:, c, :], page[i][:, first_col : first_col + P], ident[:])
+                blocks = crossed[2][:, 4 * b : 4 * (b + 1)]
+                if i == 4:
+                    nc.scalar.copy(blocks[:, :, 1, :, :], turned_rows[:].unsqueeze(3).to_broadcast([P, 4, P, 2]))
+                else:
+                    half = slice(64 * (i - 5), 64 * (i - 4))
+                    nc.scalar.copy(blocks[:, :, 0, half, :], turned_rows[:].rearrange("p c (q e) -> p c q e", e=2))
 
-        def place_third(c):
-            nc.scalar.copy(last[c][:, :, 2:4], page[6][:, chunks[c]].unsqueeze(2).to_broadcast([P, CHUNKS[c], 2]))
+        def cross_back_late():
+            words = crossed[2][:].rearrange("p b u q e -> p (b u q e)").bitcast(F32)
+            turn = 0
+            for c, width in enumerate(CHUNKS):
+                last.append(tile([P, width, 4], BF16, "woven1%d" % c, tag=WOVEN_TAGS[c]))
+                woven_words = last[c][:].rearrange("p m t -> p (m t)").bitcast(F32)
+                count = min(2, width // P)
+                for first in range(0, width // P, count):
+                    pairs = psum.tile([P, count, 2, P], F32, name="cross_back", tag="bank%d" % BACK_BANKS[turn])
+                    turn = turn + 1
+                    for b in range(count):
+                        for u in range(2):
+                            first_word = P * (2 * (edges[c] // P + first + b) + u)
+                            nc.tensor.transpose(pairs[:, b, u, :], words[:, first_word : first_word + P], ident[:])
+                    nc.scalar.copy(
+                        woven_words[:, 2 * P * first : 2 * P * (first + count)].rearrange(
+                            "p (b m u) -> p b m u", b=count, u=2
+                        ),
+                        pairs[:].rearrange("p b u m -> p b m u"),
+                    )
 
         def place_fourth(c):
             engine_copy = nc.scalar.copy if c == SCALAR_CHUNK else nc.vector.tensor_copy
@@ -304,31 +343,36 @@ def tile_list_turf_probe_page_kernel(
                     out_3[g, 4 * q : 4 * q + 4, :].bitcast(I32), scales[g][32 * q : 32 * q + 4, :].bitcast(I32)
                 )
 
-        u_first = tile([P, S], F32, "u")
+        u_first = [tile([P, BANK], F32, "u%d" % h, tag=("u", "wg3")[h]) for h in range(2)]
         first_products(0, left_half(0, 0))
-        left = {1: left_tiles(1) + (left_half(1, 0),)}
-        share(1)
+        nc.gpsimd.tensor_tensor(rt[0][:, halves[0]], u_first[0][:], wg_plain[:, halves[0]], ALU.mult)
         first_products(1, left_half(0, 1))
+        left = {1: left_tiles(1) + (left_half(1, 0),)}
         copy_half(1, 1, left_half(1, 1))
-        for h, engine in enumerate((nc.gpsimd, nc.vector)):
-            engine.tensor_tensor(rt[0][:, halves[h]], u_first[:, halves[h]], wg_plain[:, halves[h]], ALU.mult)
+        share(1)
+        scatter_half(0, 0, rt[0][:, halves[0]])
         replace(1)
-        scatter(0)
+        for a in range(2):
+            deal(0, 1, a)
+        first_high = tile([P, BANK], F32, "first_high", tag="w1head11")
+        nc.gpsimd.tensor_tensor(first_high[:], u_first[1][:], wg_plain[:, halves[1]], ALU.mult)
+        w1c[0, 1] = tile([P, 512], U32, "w1c01", tag="wg3")[:]
+        quant_w1(0, 2, 2)
+        placed[1] = tile([P, S], F32, "placed1", tag="woven1")
+        nc.gpsimd.tensor_tensor(placed[1][:], left[1][0][:], wg_plain[:], ALU.mult)
+        scatter_half(0, 1, first_high[:])
+        nc.sync.dma_start(rows(out_1, 0), page[0][:])
         copy_left(2)
         for u in range(2):
-            dealt[1, u] = tile([P, 2, 1024], BF16, "dealt1%d" % u, tag=("u", "w1head00")[u])[:]
+            dealt[1, u] = tile([P, 2, 1024], BF16, "dealt1%d" % u, tag=("w1head00", "u")[u])[:]
         for a in range(2):
             for u in range(2):
                 deal(1, u, a)
         copy_left(3)
         for c in range(8):
             nc.tensor.transpose(turned[c // 4][:, c % 4, :], wg_plain[:, P * c : P * (c + 1)], ident[:])
-        for t in range(4):
+        for t in range(3):
             turn_wg(t, spread_wg(t))
-        for i in range(6, 8):
-            rt.append(tile([P, S], F32, "right%d" % i))
-            load_right(i)
-            load_page(i)
         for q in range(4):
             nc.sync.dma_start(
                 w2s[32 * q : 32 * q + 4, :, :].bitcast(I32),
@@ -336,7 +380,7 @@ def tile_list_turf_probe_page_kernel(
             )
         for i in range(1, 8):
             if i == 7:
-                scatter_last(0)
+                scatter_half(7, 0, last_values[0])
                 codes[0] = tile([P, T2], U32, "codes0", tag="right0")
                 for c in range(2):
                     quantize_page(0, slice(1024 * c, 1024 * (c + 1)), first[c][:], codes[0][:, 1024 * c : 1024 * (c + 1)])
@@ -348,26 +392,25 @@ def tile_list_turf_probe_page_kernel(
             if i < 7:
                 scatter(i)
             else:
-                scatter_last(1)
+                scatter_half(7, 1, last_values[1])
                 nc.sync.dma_start(rows(out_1, 7), page[7][:])
             if i == 1:
                 replace(2)
-                w1c.append(tile([P, 1024], U32, "w1c1", tag="right1"))
-                w1s.append(tile([P, 1024], U8, "w1s1", tag="w1head11"))
-                quant_w1(1, 0, 2)
+                second = tile([P, 2, 512], U32, "w1c1", tag="woven14")
+                w1c[1, 0], w1c[1, 1] = second[:, 0, :], second[:, 1, :]
+                w1s.append(tile([P, 1024], U8, "w1s1", tag="right1"))
                 quant_w1(1, 2, 2)
+                quant_w1(1, 0, 2)
             elif i < 7:
                 replace(i + 1)
             if i + 3 < 8:
                 copy_left(i + 3)
             if i <= 4:
                 cross(i - 1)
-            for b in range(4 if i in (5, 6) else 0):
-                round_plane(i - 1, slice(BANK * b, BANK * (b + 1)), nc.scalar.copy)
-            for c in range(len(CHUNKS) if i == 6 else 0):
-                place_low_pair(c)
-            for c in range(len(CHUNKS) if i == 7 else 0):
-                place_third(c)
+            else:
+                cross_late(i - 1)
+            if i == 7:
+                cross_back_late()
             if i == 4:
                 first = [tile([P, 4096], BF16, "woven0%d" % c, tag="tabw%d" % c) for c in range(2)]
                 for c in range(2):
@@ -378,7 +421,8 @@ def tile_list_turf_probe_page_kernel(
 
         def product(k, g):
             c, n0, count = units[k]
-            if g == 0:
+            opening = 0 if k < AHEAD else 1
+            if g == opening:
                 accs[k] = psum.tile([P, count, CHUNKS[c]], F32, name="prod", tag="bank%d" % (k % 8))
             for n in range(n0, n0 + count):
                 nc.tensor.matmul_mx(
@@ -387,11 +431,11 @@ def tile_list_turf_probe_page_kernel(
                     lhsT_scale=w2s[:, g, P * n : P * (n + 1)],
                     rhs=(codes[0][:, chunks[c]] if g == 0 else last_codes[c][:]).bitcast(FP8X4),
                     rhs_scale=scales[g][:, chunks[c]],
-                    start=(g == 0 and n == n0),
-                    stop=(g == 1 and n == n0 + count - 1),
+                    start=(g == opening and n == n0),
+                    stop=(g != opening and n == n0 + count - 1),
                 )
 
-        for k in range(8):
+        for k in range(AHEAD):
             product(k, 0)
 
         last_codes = [tile([P, w], U32, "codes1%d" % c, tag=CODE_TAGS[c]) for c, w in enumerate(CHUNKS)]
@@ -416,6 +460,9 @@ def tile_list_turf_probe_page_kernel(
 
         for k in range(8):
             product(k, 1)
+            if k >= AHEAD:
+                product(k, 0)
+
         def values(k):
             c, n0, count = units[k]
             first_col = edges[c] % BANK
@@ -446,8 +493,8 @@ def tile_list_turf_probe_page_kernel(
             finish_bank(k)
         for k in range(ON_SCALAR, 16):
             if k >= 8:
-                product(k, 0)
                 product(k, 1)
+                product(k, 0)
             square_bank(k)
         for k in FINISH_ORDER:
             finish_bank(k)

@@ -26,14 +26,15 @@ WORK_TAGS = {1: "u", 2: "right1", 3: "w1head00", 4: "w1head00", 5: "w1c0", 6: "w
 SQUARE_TAGS = {1: "woven14", 4: "w1c0", 7: "w1head00"}
 CHUNKS = (128, 128, 256, 512, 512, 512)
 WOVEN_TAGS = ("right2", "right3", "right4", "right5", "woven14", "square2")
-CODE_TAGS = ("w1s0", "gw0", "gw1", "w1c0", "right1", "square0")
 BACK_BANKS = (4, 5, 6, 7, 4, 3, 2, 1, 0)
 AHEAD = 4
+CODE_TAGS = ("gw0", "w1c0", "right1", "square0")
 SCALAR_CHUNK = 5
 ROLES = "SSSSSSSGGGVGVGVV"
 ON_SCALAR = 7
 FINISH_ORDER = (7, 8, 10, 9, 12, 11, 14, 13, 15)
 STORES = {2: (0, 2), 3: (2, 4), 4: (0, 1), 5: (1, 2), 6: (2, 3), 7: (3, 4), 8: (0, 1), 9: (1, 2), 10: (2, 3), 11: (3, 4), 12: (0, 1), 13: (1, 2), 14: (2, 3), 15: (3, 4)}
+CODE_STORES = {2: slice(0, 512), 3: slice(512, 1024), 4: slice(1024, 1536), 5: slice(1536, 2048)}
 
 
 def tile_list_turf_probe_page_kernel(
@@ -240,14 +241,6 @@ def tile_list_turf_probe_page_kernel(
             square, plain = left[i][0], left[i][1]
             own = halves[1] if i in SHARED else slice(0, S)
             u = tile([P, S], F32, "work", tag=WORK_TAGS[i])
-            if i == 7:
-                last_values.append(tile([P, BANK], F32, "last_low", tag="right0")[:])
-                last_values.append(rt[i][:, halves[1]])
-                for h, cols in enumerate(halves):
-                    nc.gpsimd.tensor_tensor(u[:, cols], square[:, cols], rt[i][:, cols], ALU.mult)
-                    nc.gpsimd.tensor_tensor(u[:, cols], u[:, cols], plain[:, cols], ALU.subtract)
-                    nc.gpsimd.tensor_tensor(last_values[h], u[:, cols], factor(i)[:, cols], ALU.mult)
-                return
             nc.gpsimd.tensor_tensor(u[:, own], square[:, own], rt[i][:, own], ALU.mult)
             if i in SHARED:
                 nc.gpsimd.tensor_tensor(square[:, own], u[:, own], plain[:, own], ALU.subtract)
@@ -255,7 +248,10 @@ def tile_list_turf_probe_page_kernel(
                     nc.gpsimd.tensor_tensor(rt[i][:], square[:], factor(i), ALU.mult)
             else:
                 nc.gpsimd.tensor_tensor(u[:], u[:], plain[:], ALU.subtract)
-                nc.gpsimd.tensor_tensor(rt[i][:], u[:], factor(i), ALU.mult)
+                if i < 7:
+                    nc.gpsimd.tensor_tensor(rt[i][:], u[:], factor(i), ALU.mult)
+                else:
+                    last_values.append(u[:])
 
         crossed = {}
 
@@ -333,9 +329,18 @@ def tile_list_turf_probe_page_kernel(
         codes = {}
         scales = [tile([P, T2], U8, "scales%d" % g) for g in range(2)]
 
-        def quantize_page(g, cols, woven, words):
-            nc.vector.quantize_mx(out=words.bitcast(FP8X4), scales=scales[g][:, cols], in_=woven)
-            nc.sync.dma_start(out_2[g].rearrange("p m t -> p (m t)").bitcast(I32)[:, cols], words.bitcast(I32))
+        def page_codes(g, cols):
+            if g == 0:
+                return codes[0][:, cols]
+            first_col = BANK * (cols.start // BANK)
+            return last_codes[cols.start // BANK][:, cols.start - first_col : cols.stop - first_col]
+
+        def quantize_page(g, cols, woven):
+            nc.vector.quantize_mx(out=page_codes(g, cols).bitcast(FP8X4), scales=scales[g][:, cols], in_=woven)
+
+        def store_codes(g, cols):
+            rows_out2 = out_2[g].rearrange("p m t -> p (m t)").bitcast(I32)
+            nc.sync.dma_start(rows_out2[:, cols], page_codes(g, cols).bitcast(I32))
 
         def store_scales(g):
             for q in range(4):
@@ -380,10 +385,10 @@ def tile_list_turf_probe_page_kernel(
             )
         for i in range(1, 8):
             if i == 7:
-                scatter_half(7, 0, last_values[0])
-                codes[0] = tile([P, T2], U32, "codes0", tag="right0")
+                codes[0] = tile([P, T2], U32, "codes0", tag="right6")
                 for c in range(2):
-                    quantize_page(0, slice(1024 * c, 1024 * (c + 1)), first[c][:], codes[0][:, 1024 * c : 1024 * (c + 1)])
+                    quantize_page(0, slice(S * c, S * (c + 1)), first[c][:])
+                    store_codes(0, slice(S * c, S * (c + 1)))
                 store_scales(0)
             if i == 3:
                 w2w = tile([P, 2, 2 * N], U8, "w2w", tag="wg_plain")
@@ -392,7 +397,7 @@ def tile_list_turf_probe_page_kernel(
             if i < 7:
                 scatter(i)
             else:
-                scatter_half(7, 1, last_values[1])
+                nc.vector.tensor_tensor(page[7][:].indirect(idx2[:]), last_values[0], factor(7), ALU.mult)
                 nc.sync.dma_start(rows(out_1, 7), page[7][:])
             if i == 1:
                 replace(2)
@@ -429,7 +434,7 @@ def tile_list_turf_probe_page_kernel(
                     out=accs[k][:, n - n0, :],
                     lhsT=w2w[:, g, 2 * P * n : 2 * P * (n + 1)].bitcast(FP4X4),
                     lhsT_scale=w2s[:, g, P * n : P * (n + 1)],
-                    rhs=(codes[0][:, chunks[c]] if g == 0 else last_codes[c][:]).bitcast(FP8X4),
+                    rhs=page_codes(g, chunks[c]).bitcast(FP8X4),
                     rhs_scale=scales[g][:, chunks[c]],
                     start=(g == opening and n == n0),
                     stop=(g != opening and n == n0 + count - 1),
@@ -438,14 +443,16 @@ def tile_list_turf_probe_page_kernel(
         for k in range(AHEAD):
             product(k, 0)
 
-        last_codes = [tile([P, w], U32, "codes1%d" % c, tag=CODE_TAGS[c]) for c, w in enumerate(CHUNKS)]
+        last_codes = [tile([P, BANK], U32, "codes1%d" % b, tag=CODE_TAGS[b]) for b in range(4)]
         place_fourth(SCALAR_CHUNK)
         ahead = [c for c in range(len(CHUNKS)) if c != SCALAR_CHUNK]
         place_fourth(ahead[0])
         for c, cols in enumerate(chunks):
             if c + 1 < len(ahead):
                 place_fourth(ahead[c + 1])
-            quantize_page(1, cols, last[c][:].rearrange("p m t -> p (m t)"), last_codes[c][:])
+            quantize_page(1, cols, last[c][:].rearrange("p m t -> p (m t)"))
+            if c in CODE_STORES:
+                store_codes(1, CODE_STORES[c])
         store_scales(1)
 
         rows_out0 = out_0.rearrange("(n p) m -> p n m", p=P)

from contextlib import ExitStack

import concourse.mybir as mybir
from concourse.masks import make_identity

K, H, N, T, S, T2 = 1024, 1024, 512, 2048, 1024, 2048
FLOPS = 2 * K * H * S + 2 * H * N * T2

F32 = mybir.dt.float32
BF16 = mybir.dt.bfloat16
I32 = mybir.dt.int32
U32 = mybir.dt.uint32
U16 = mybir.dt.uint16
U8 = mybir.dt.uint8
FP8X4 = mybir.dt.float8_e4m3fn_x4
FP4X4 = mybir.dt.float4_e2m1fn_x4
ALU = mybir.AluOpType
ACT = mybir.ActivationFunctionType

P = 128
BANK = 512
SHARED = {1: "square0", 4: "right2"}
PLACES = {4: (1, 0), 5: (0, 0), 6: (0, 1), 7: (1, 1)}
FACTORS = {4: 0, 5: 1, 6: 1, 7: 2}
WORK_TAGS = {1: "u", 2: "right1", 3: "w1head00", 4: "w1head00", 5: "w1c0", 6: "w1c0", 7: "w1c0"}
SQUARE_TAGS = {1: "woven14", 4: "w1c0", 7: "w1head00"}
CHUNKS = (128, 128, 256, 512, 512, 512)
WOVEN_TAGS = ("right2", "right3", "right4", "right5", "woven14", "square2")
BACK_BANKS = (4, 5, 6, 7, 4, 3, 2, 1, 0)
AHEAD = 4
CODE_TAGS = ("gw0", "w1c0", "right1", "square0")
SCALAR_CHUNK = 5
ROLES = "SSSSSSSGGGVGVGVV"
ON_SCALAR = 7
FINISH_ORDER = (7, 8, 10, 9, 12, 11, 14, 13, 15)
STORES = {2: (0, 2), 3: (2, 4), 4: (0, 1), 5: (1, 2), 6: (2, 3), 7: (3, 4), 8: (0, 1), 9: (1, 2), 10: (2, 3), 11: (3, 4), 12: (0, 1), 13: (1, 2), 14: (2, 3), 15: (3, 4)}
CODE_STORES = {2: slice(0, 512), 3: slice(512, 1024), 4: slice(1024, 1536), 5: slice(1536, 2048)}


def tile_list_turf_probe_page_kernel(
    tc, tab_words, tab_scales, offs, offs2, w1, right, wgs, page0, w2_words, w2_scales, out_0, out_1, out_2, out_3
):
    nc = tc.nc
    with ExitStack() as ctx:
        lists = ctx.enter_context(tc.tile_pool(name="lists", bufs=1))
        sb = ctx.enter_context(tc.tile_pool(name="sb", bufs=1))
        ring = ctx.enter_context(tc.tile_pool(name="ring", bufs=3))
        psum = ctx.enter_context(tc.psum_pool(name="psum", bufs=1))

        def tile(shape, dtype, name, tag=None):
            return sb.tile(shape, dtype, name=name, tag=tag or name, align_bytes=64)

        idx = lists.tile([P, S // 16], U16, name="idx")
        idx2 = lists.tile([P, S // 16], U16, name="idx2")
        tabw = [tile([P, T], U32, "tabw%d" % a) for a in range(2)]
        tabs = tile([P, T], U8, "tabs")
        w1head = {(u, a): tile([P, 4, 256], F32, "w1head%d%d" % (u, a)) for u in range(2) for a in range(2)}
        w1raw = [tile([P, 4, 512], F32, "w1raw1%d" % a) for a in range(2)]
        rt = [tile([P, S], F32, "right%d" % i) for i in range(8)]
        wg = [tile([P, S], F32, "wg%d" % t) for t in range(3)]
        page = [tile([P, T2], F32, "page%d" % i) for i in range(8)]
        w2s = tile([P, 2, N], U8, "w2s")
        warm = tile([P, 1], F32, "warm")
        ident = tile([P, P], F32, "ident")
        wg_plain = tile([P, S], F32, "wg_plain")

        def rows(matrix, i):
            if i < 4:
                return matrix[P * i : P * (i + 1), :]
            if i in (5, 6):
                return matrix[256 * (i - 3) : 256 * (i - 2), :].rearrange("(p t) m -> p t m", t=4)[:, 0:2, :]
            return matrix[512:1024, :].rearrange("(p t) m -> t p m", t=4)[2 if i == 4 else 3]

        nc.vector.memset(tabs[:].bitcast(I32), 0)
        nc.vector.memset(warm[:], 1.0)
        nc.vector.memset(w2s[:].rearrange("p a c -> p (a c)").bitcast(I32), 0)
        nc.scalar.activation(warm[:], warm[:], ACT.Ln)

        def load_tabw(a):
            nc.sync.dma_start(tabw[a][:].bitcast(I32), tab_words[a].rearrange("p t i -> p (t i)").bitcast(I32))

        def load_w1(dst, a, cols):
            nc.sync.dma_start(dst[:], w1[512 * a : 512 * (a + 1), cols].rearrange("(p j) c -> p j c", j=4))

        def load_right(i):
            nc.sync.dma_start(rt[i][:], rows(right, i))

        def load_page(i):
            nc.sync.dma_start(page[i][:], rows(page0, i))

        load_tabw(0)
        nc.sync.dma_start(idx[:], offs)
        load_tabw(1)
        for q in range(4):
            nc.gpsimd.dma_start(
                tabs[32 * q : 32 * q + 8, :].bitcast(I32), tab_scales[:, 4 * q : 4 * q + 4, :].bitcast(I32)
            )
        make_identity(nc, ident[:])
        for a in range(2):
            load_w1(w1head[0, a], a, slice(0, 256))
        halves = [slice(0, BANK), slice(BANK, S)]
        load_right(0)
        nc.sync.dma_start(wg_plain[:, halves[0]], wgs[:, halves[0]])
        load_right(1)
        nc.sync.dma_start(idx2[:], offs2)
        load_page(0)
        for a in range(2):
            load_w1(w1head[1, a], a, slice(256, 512))
        nc.sync.dma_start(wg_plain[:, halves[1]], wgs[:, halves[1]])
        load_right(2)
        load_page(1)
        for a in range(2):
            load_w1(w1raw[a], a, slice(512, 1024))
        for i in range(3, 8):
            load_right(i)
            load_page(i - 1)
        load_page(7)

        turned = [psum.tile([P, 4, P], F32, name="turned", tag="bank%d" % (6 + h)) for h in range(2)]

        def spread_wg(t):
            spread = tile([P, 8, P], F32, "spread", tag="w1head10")
            for h in range(2):
                part = spread[:, 4 * h : 4 * (h + 1), :]
                if t == 1:
                    picked = turned[h][:].rearrange("p c (q t) -> p c q t", t=4)[:, :, :, 0:2]
                    nc.scalar.copy(
                        part.rearrange("p c (a q e) -> p c a q e", a=2, e=2),
                        picked.unsqueeze(2).to_broadcast([P, 4, 2, 32, 2]),
                    )
                else:
                    picked = turned[h][:].rearrange("p c (q t) -> p c t q", t=4)[:, :, 2 + t // 2 : 3 + t // 2, :]
                    nc.scalar.copy(part.rearrange("p c (a q) -> p c a q", a=4), picked.to_broadcast([P, 4, 4, 32]))
            return spread

        def turn_wg(t, spread):
            for h in range(2):
                back = psum.tile([P, 4, P], F32, name="back", tag="bank%d" % (4 + h))
                for c in range(4):
                    nc.tensor.transpose(back[:, c, :], spread[:, 4 * h + c, :], ident[:])
                nc.scalar.copy(wg[t][:, halves[h]], back[:].rearrange("p c j -> p (c j)"))

        gw = [tile([P, S], U32, "gw%d" % a) for a in range(2)]
        for a in range(2):
            nc.vector.tensor_copy(gw[a][:], tabw[a][:].indirect(idx[:]))
        gs = {}

        def gather_scales(h):
            gs[h] = tile([P, BANK], U8, "gs%d" % h, tag=("tabw1", "w1head01")[h])
            nc.vector.tensor_copy(gs[h][:], tabs[:].indirect(idx[:, 32 * h : 32 * (h + 1)]))

        dealt = {(0, u): tile([P, 2, 1024], BF16, "dealt0%d" % u, tag=("square0", "woven1")[u])[:] for u in range(2)}
        w1c = {(0, 0): tile([P, 512], U32, "w1c0")[:]}
        w1s = [tile([P, 1024], U8, "w1s0")]

        def deal(g, u, a):
            if g == 0:
                dst = dealt[g, u][:, a, :].rearrange("p (c i j) -> p c j i", i=4, j=4)
                src = w1head[u, a][:].rearrange("p j (c i) -> p c j i", i=4)
            else:
                dst = dealt[g, u][:, a, :].rearrange(("p (m t j) -> p m j t", "p (t m j) -> p m j t")[u], t=2, j=4)
                src = w1raw[a][:].rearrange("p j (m t) -> p m j t", t=4)[:, :, :, 2 * u : 2 * u + 2]
            nc.scalar.copy(dst, src)

        def quant_w1(g, first, count):
            cols = slice(256 * first, 256 * (first + count))
            nc.vector.quantize_mx(
                out=w1c[g, first // 2][:, 256 * (first % 2) : 256 * (first % 2 + count)].bitcast(FP8X4),
                scales=w1s[g][:, cols],
                in_=dealt[g, first // 2].rearrange("p a c -> p (a c)")[:, 1024 * (first % 2) : 1024 * (first % 2 + count)],
            )

        deal(0, 0, 0)
        quant_w1(0, 0, 1)
        gather_scales(0)
        deal(0, 0, 1)
        quant_w1(0, 1, 1)
        gather_scales(1)

        def left_half(i, h):
            g = i // 4
            u, e = PLACES.get(i, (i // 2, i % 2))
            acc = psum.tile([P, BANK], F32, name="left", tag="bank%d" % (2 * (i % 2) + h))
            for a in range(2):
                cols = slice(512 * u + 256 * a + P * e, 512 * u + 256 * a + P * (e + 1))
                nc.tensor.matmul_mx(
                    out=acc[:],
                    lhsT=w1c[g, u][:, 256 * a + P * e : 256 * a + P * (e + 1)].bitcast(FP8X4),
                    lhsT_scale=w1s[g][:, cols],
                    rhs=gw[a][:, halves[h]].bitcast(FP8X4),
                    rhs_scale=gs[h][4 * a : P, :],
                    start=(a == 0),
                    stop=(a == 1),
                )
            return acc

        def left_tiles(i):
            square = tile([P, S], F32, "square", tag=SQUARE_TAGS.get(i, "square%d" % (i % 3)))
            plain = ring.tile([P, S], F32, name="plain", tag="plain", align_bytes=64)
            return square, plain

        def copy_half(i, h, bank):
            square, plain = left[i][0], left[i][1]
            nc.scalar.activation(square[:, halves[h]], bank[:], ACT.Square)
            nc.scalar.copy(plain[:, halves[h]], bank[:])

        def copy_left(i):
            banks = [left_half(i, h) for h in range(2)]
            left[i] = left_tiles(i) + (banks[0],)
            own = range(1 if i in SHARED else 0, 2)
            for h in own:
                nc.scalar.activation(left[i][0][:, halves[h]], banks[h][:], ACT.Square)
            for h in own:
                nc.scalar.copy(left[i][1][:, halves[h]], banks[h][:])

        def factor(i):
            return wg_plain[:] if i < 4 else wg[FACTORS[i]][:]

        placed = {}

        def scatter(i):
            nc.vector.tensor_copy(page[i][:].indirect(idx2[:]), placed.get(i, rt[i])[:])
            nc.sync.dma_start(rows(out_1, i), page[i][:])

        def scatter_half(i, h, part):
            nc.vector.tensor_copy(page[i][:].indirect(idx2[:, 32 * h : 32 * (h + 1)]), part)

        def first_products(h, bank):
            nc.vector.tensor_tensor(u_first[h][:], bank[:], rt[0][:, halves[h]], ALU.mult)
            nc.vector.scalar_tensor_tensor(u_first[h][:], u_first[h][:], -1.0, bank[:], ALU.add, ALU.mult)

        def share(i):
            square, bank = left[i][0], left[i][2]
            shared = tile([P, BANK], F32, "shared%d" % i, tag=SHARED[i])
            nc.vector.tensor_tensor(shared[:], bank[:], rt[i][:, halves[0]], ALU.mult)
            nc.vector.scalar_tensor_tensor(square[:, halves[0]], shared[:], -1.0, bank[:], ALU.add, ALU.mult)

        last_values = []

        def replace(i):
            square, plain = left[i][0], left[i][1]
            own = halves[1] if i in SHARED else slice(0, S)
            u = tile([P, S], F32, "work", tag=WORK_TAGS[i])
            nc.gpsimd.tensor_tensor(u[:, own], square[:, own], rt[i][:, own], ALU.mult)
            if i in SHARED:
                nc.gpsimd.tensor_tensor(square[:, own], u[:, own], plain[:, own], ALU.subtract)
                if i > 1:
                    nc.gpsimd.tensor_tensor(rt[i][:], square[:], factor(i), ALU.mult)
            else:
                nc.gpsimd.tensor_tensor(u[:], u[:], plain[:], ALU.subtract)
                if i < 7:
                    nc.gpsimd.tensor_tensor(rt[i][:], u[:], factor(i), ALU.mult)
                else:
                    last_values.append(u[:])

        crossed = {}

        edges = [sum(CHUNKS[:c]) for c in range(len(CHUNKS) + 1)]
        chunks = [slice(edges[c], edges[c + 1]) for c in range(len(CHUNKS))]
        last = []

        def cross_late(i):
            if i == 4:
                crossed[2] = tile([P, 16, 2, P, 2], BF16, "crossed2", tag="woven1")
            for b in range(4):
                turned_rows = psum.tile([P, 4, P], F32, name="cross", tag="bank%d" % (4 + b))
                for c in range(4):
                    first_col = BANK * b + P * c
                    nc.tensor.transpose(turned_rows[:, c, :], page[i][:, first_col : first_col + P], ident[:])
                blocks = crossed[2][:, 4 * b : 4 * (b + 1)]
                if i == 4:
                    nc.scalar.copy(blocks[:, :, 1, :, :], turned_rows[:].unsqueeze(3).to_broadcast([P, 4, P, 2]))
                else:
                    half = slice(64 * (i - 5), 64 * (i - 4))
                    nc.scalar.copy(blocks[:, :, 0, half, :], turned_rows[:].rearrange("p c (q e) -> p c q e", e=2))

        def cross_back_late():
            words = crossed[2][:].rearrange("p b u q e -> p (b u q e)").bitcast(F32)
            turn = 0
            for c, width in enumerate(CHUNKS):
                last.append(tile([P, width, 4], BF16, "woven1%d" % c, tag=WOVEN_TAGS[c]))
                woven_words = last[c][:].rearrange("p m t -> p (m t)").bitcast(F32)
                count = min(2, width // P)
                for first in range(0, width // P, count):
                    pairs = psum.tile([P, count, 2, P], F32, name="cross_back", tag="bank%d" % BACK_BANKS[turn])
                    turn = turn + 1
                    for b in range(count):
                        for u in range(2):
                            first_word = P * (2 * (edges[c] // P + first + b) + u)
                            nc.tensor.transpose(pairs[:, b, u, :], words[:, first_word : first_word + P], ident[:])
                    nc.scalar.copy(
                        woven_words[:, 2 * P * first : 2 * P * (first + count)].rearrange(
                            "p (b m u) -> p b m u", b=count, u=2
                        ),
                        pairs[:].rearrange("p b u m -> p b m u"),
                    )

        def place_fourth(c):
            engine_copy = nc.scalar.copy if c == SCALAR_CHUNK else nc.vector.tensor_copy
            engine_copy(last[c][:, :, 3], page[7][:, chunks[c]])

        def cross(i):
            for b in range(4):
                if b // 2 not in crossed:
                    crossed[b // 2] = tile([P, 8, 2, 4, 32, 2], BF16, "crossed%d" % (b // 2), tag=("w1raw11", "u")[b // 2])
                turned_rows = psum.tile([P, 4, P], F32, name="cross", tag="bank%d" % (4 + b))
                for c in range(4):
                    first_col = BANK * b + P * c
                    nc.tensor.transpose(turned_rows[:, c, :], page[i][:, first_col : first_col + P], ident[:])
                nc.scalar.copy(
                    crossed[b // 2][:, 4 * (b % 2) : 4 * (b % 2 + 1), :, i, :, :],
                    turned_rows[:].rearrange("p c (q u e) -> p c u q e", u=2, e=2),
                )

        def cross_back(woven, half):
            words = crossed[half][:].rearrange("p c u i q e -> p (c u i q e)").bitcast(F32)
            woven_words = woven.bitcast(F32)
            for b in range(4):
                pairs = psum.tile([P, 2, 2, P], F32, name="cross_back", tag="bank%d" % (4 + b))
                for c in range(2):
                    for u in range(2):
                        first_word = P * (2 * (2 * b + c) + u)
                        nc.tensor.transpose(pairs[:, c, u, :], words[:, first_word : first_word + P], ident[:])
                nc.scalar.copy(
                    woven_words[:, 512 * b : 512 * (b + 1)].rearrange("p (c m u) -> p c m u", c=2, u=2),
                    pairs[:].rearrange("p c u m -> p c m u"),
                )

        codes = {}
        scales = [tile([P, T2], U8, "scales%d" % g) for g in range(2)]

        def page_codes(g, cols):
            if g == 0:
                return codes[0][:, cols]
            first_col = BANK * (cols.start // BANK)
            return last_codes[cols.start // BANK][:, cols.start - first_col : cols.stop - first_col]

        def quantize_page(g, cols, woven):
            nc.vector.quantize_mx(out=page_codes(g, cols).bitcast(FP8X4), scales=scales[g][:, cols], in_=woven)

        def store_codes(g, cols):
            rows_out2 = out_2[g].rearrange("p m t -> p (m t)").bitcast(I32)
            nc.sync.dma_start(rows_out2[:, cols], page_codes(g, cols).bitcast(I32))

        def store_scales(g):
            for q in range(4):
                nc.sync.dma_start(
                    out_3[g, 4 * q : 4 * q + 4, :].bitcast(I32), scales[g][32 * q : 32 * q + 4, :].bitcast(I32)
                )

        u_first = [tile([P, BANK], F32, "u%d" % h, tag=("u", "wg3")[h]) for h in range(2)]
        first_products(0, left_half(0, 0))
        nc.gpsimd.tensor_tensor(rt[0][:, halves[0]], u_first[0][:], wg_plain[:, halves[0]], ALU.mult)
        first_products(1, left_half(0, 1))
        left = {1: left_tiles(1) + (left_half(1, 0),)}
        copy_half(1, 1, left_half(1, 1))
        share(1)
        scatter_half(0, 0, rt[0][:, halves[0]])
        replace(1)
        for a in range(2):
            deal(0, 1, a)
        first_high = tile([P, BANK], F32, "first_high", tag="w1head11")
        nc.gpsimd.tensor_tensor(first_high[:], u_first[1][:], wg_plain[:, halves[1]], ALU.mult)
        w1c[0, 1] = tile([P, 512], U32, "w1c01", tag="wg3")[:]
        quant_w1(0, 2, 2)
        placed[1] = tile([P, S], F32, "placed1", tag="woven1")
        nc.gpsimd.tensor_tensor(placed[1][:], left[1][0][:], wg_plain[:], ALU.mult)
        scatter_half(0, 1, first_high[:])
        nc.sync.dma_start(rows(out_1, 0), page[0][:])
        copy_left(2)
        for u in range(2):
            dealt[1, u] = tile([P, 2, 1024], BF16, "dealt1%d" % u, tag=("w1head00", "u")[u])[:]
        for a in range(2):
            for u in range(2):
                deal(1, u, a)
        copy_left(3)
        for c in range(8):
            nc.tensor.transpose(turned[c // 4][:, c % 4, :], wg_plain[:, P * c : P * (c + 1)], ident[:])
        for t in range(3):
            turn_wg(t, spread_wg(t))
        for q in range(4):
            nc.sync.dma_start(
                w2s[32 * q : 32 * q + 4, :, :].bitcast(I32),
                w2_scales[:, 4 * q : 4 * q + 4, :].rearrange("a r c -> r a c").bitcast(I32),
            )
        for i in range(1, 8):
            if i == 7:
                codes[0] = tile([P, T2], U32, "codes0", tag="right6")
                for c in range(2):
                    quantize_page(0, slice(S * c, S * (c + 1)), first[c][:])
                    store_codes(0, slice(S * c, S * (c + 1)))
                store_scales(0)
            if i == 3:
                w2w = tile([P, 2, 2 * N], U8, "w2w", tag="wg_plain")
                nc.sync.dma_start(w2w[:].bitcast(I32), w2_words.rearrange("a p c -> p a c").bitcast(I32))
                share(4)
            if i < 7:
                scatter(i)
            else:
                nc.vector.tensor_tensor(page[7][:].indirect(idx2[:]), last_values[0], factor(7), ALU.mult)
                nc.sync.dma_start(rows(out_1, 7), page[7][:])
            if i == 1:
                replace(2)
                second = tile([P, 2, 512], U32, "w1c1", tag="woven14")
                w1c[1, 0], w1c[1, 1] = second[:, 0, :], second[:, 1, :]
                w1s.append(tile([P, 1024], U8, "w1s1", tag="right1"))
                quant_w1(1, 2, 2)
                quant_w1(1, 0, 2)
            elif i < 7:
                replace(i + 1)
            if i + 3 < 8:
                copy_left(i + 3)
            if i <= 4:
                cross(i - 1)
            else:
                cross_late(i - 1)
            if i == 7:
                cross_back_late()
            if i == 4:
                first = [tile([P, 4096], BF16, "woven0%d" % c, tag="tabw%d" % c) for c in range(2)]
                for c in range(2):
                    cross_back(first[c][:], c)

        units = [(c, n0, BANK // w) for c, w in enumerate(CHUNKS) for n0 in range(0, 4, BANK // w)]
        accs = {}

        def product(k, g):
            c, n0, count = units[k]
            opening = 0 if k < AHEAD else 1
            if g == opening:
                accs[k] = psum.tile([P, count, CHUNKS[c]], F32, name="prod", tag="bank%d" % (k % 8))
            for n in range(n0, n0 + count):
                nc.tensor.matmul_mx(
                    out=accs[k][:, n - n0, :],
                    lhsT=w2w[:, g, 2 * P * n : 2 * P * (n + 1)].bitcast(FP4X4),
                    lhsT_scale=w2s[:, g, P * n : P * (n + 1)],
                    rhs=page_codes(g, chunks[c]).bitcast(FP8X4),
                    rhs_scale=scales[g][:, chunks[c]],
                    start=(g == opening and n == n0),
                    stop=(g != opening and n == n0 + count - 1),
                )

        for k in range(AHEAD):
            product(k, 0)

        last_codes = [tile([P, BANK], U32, "codes1%d" % b, tag=CODE_TAGS[b]) for b in range(4)]
        place_fourth(SCALAR_CHUNK)
        ahead = [c for c in range(len(CHUNKS)) if c != SCALAR_CHUNK]
        place_fourth(ahead[0])
        for c, cols in enumerate(chunks):
            if c + 1 < len(ahead):
                place_fourth(ahead[c + 1])
            quantize_page(1, cols, last[c][:].rearrange("p m t -> p (m t)"))
            if c in CODE_STORES:
                store_codes(1, CODE_STORES[c])
        store_scales(1)

        rows_out0 = out_0.rearrange("(n p) m -> p n m", p=P)
        early = tile([P, 4, BANK], F32, "staged_early", tag="w1raw10")
        middle = tile([P, 4, BANK], F32, "staged_middle", tag="w1raw11")
        late = tile([P, 8, BANK], F32, "staged_late", tag="woven1")

        def staged(k, first_row, stop_row):
            home, base = (early, 0) if k < 4 else (middle, 4) if k < 8 else (late, 8)
            row0 = 4 * (k // 4) - base
            return home[:, row0 + first_row : row0 + stop_row, :]

        for k in range(8):
            product(k, 1)
            if k >= AHEAD:
                product(k, 0)

        def values(k):
            c, n0, count = units[k]
            first_col = edges[c] % BANK
            return staged(k, n0, n0 + count)[:, :, first_col : first_col + CHUNKS[c]]

        def square_bank(k):
            y, acc = values(k), accs[k][:]
            if ROLES[k] == "S":
                nc.scalar.activation(y, acc, ACT.Square)
            elif ROLES[k] == "G":
                nc.vector.tensor_copy(y, acc)
                nc.gpsimd.tensor_tensor(y, y, y, ALU.mult)
            else:
                nc.vector.tensor_copy(y, acc)
                nc.vector.tensor_tensor(y, acc, y, ALU.mult)

        def finish_bank(k):
            nc.scalar.activation(values(k), values(k), ACT.Ln, bias=1.0)
            if k in STORES:
                first_row, stop_row = STORES[k]
                block = k // 4
                nc.sync.dma_start(
                    rows_out0[:, first_row:stop_row, BANK * block : BANK * (block + 1)], staged(k, first_row, stop_row)
                )

        for k in range(ON_SCALAR):
            square_bank(k)
            finish_bank(k)
        for k in range(ON_SCALAR, 16):
            if k >= 8:
                product(k, 1)
                product(k, 0)
            square_bank(k)
        for k in FINISH_ORDER:
            finish_bank(k)
